import numpy as np, ml_dtypes
CORES = [2,3,42,43,82,83,122,123]
N = 8
BF = ml_dtypes.bfloat16
S, NM, L, RO, TAU = 2048, 4096, 128, 4, 4
ST, C0, LN = S // L, 16 - RO, NM.bit_length() - 1
def pack(nm, st, kd, ac, fu):
    return np.where(fu, 1 + 2048 * nm + 32 * st + 16 * kd + ac, 0)
def done(e, x, w, kp):
    return {"ent": np.ascontiguousarray(e.reshape(N, 128, S)).astype(np.int32), "feat": np.ascontiguousarray(x.reshape(N, 128, NM)).astype(np.float32).astype(BF),
            "wt": np.ascontiguousarray(w.reshape(N, 128, 1)).astype(np.int32), "kap": np.ascontiguousarray(kp.reshape(N, 128, 1)).astype(np.int32)}
def pooled(rng, n, other):
    pool = rng.integers(0, NM, (8, 16, n)); pool[..., 0] = rng.choice(np.array([0, NM - 1]), (8, 16))
    j = (n * rng.random((N, 8, 16, S)) ** 2).astype(np.int64)
    v = pool[np.arange(8)[:, None, None], np.arange(16)[None, :, None], j]
    return np.where(rng.random(v.shape) < other, rng.integers(0, NM, v.shape), v)
def parts(rng, n, other):
    sh = (N, 8, 16, S); nm = pooled(rng, n, other)
    st = rng.integers(0, 64, sh); kd = (rng.random(sh) < 0.45).astype(np.int64); ac = rng.integers(0, 16, sh); fu = rng.random(sh) < 0.8
    x = (64 * rng.random((N, 8, 16, NM)) ** 2).astype(np.int64)
    return nm, st, kd, ac, fu, x, rng.integers(0, 256, (N, 8, 16)), rng.integers(0, 256, (N, 8, 16))
def setup_inputs(rng):
    nm, st, kd, ac, fu, x, w, kp = parts(rng, 24, 0.3)
    return done(pack(nm, st, kd, ac, fu), x, w, kp)
def setup_inputs_spread(rng):
    sh = (N, 8, 16, S)
    nm = np.exp2(LN * rng.random(sh)).astype(np.int64) - 1; nm = np.where(rng.random((1, 8, 16, 1)) < 0.5, NM - 1 - nm, nm)
    st = np.exp2(6 * rng.random(sh)).astype(np.int64) - 1; st = np.where(rng.random(sh) < 0.5, 63 - st, st)
    kd = (rng.random(sh) < rng.choice(np.array([0.1, 0.4, 0.8]), (N, 8, 1, 1))).astype(np.int64)
    fu = rng.random(sh) < rng.random((N, 8, 1, S))
    x = (np.exp2(6 * rng.random((N, 8, 1, NM))) * rng.random((N, 8, 16, NM))).astype(np.int64)
    w = np.exp2(8 * rng.random((N, 8, 16))).astype(np.int64) - 1; kp = 256 - np.exp2(8 * rng.random((N, 8, 16))).astype(np.int64)
    return done(pack(nm, st, kd, rng.integers(0, 16, sh), fu), x, w, kp)
def at_ends(rng, hi):
    o = np.argsort(rng.random((N, 8, 16)), axis=-1)
    return np.where(o < 11, hi * rng.integers(0, 2, o.shape), rng.integers(0, hi + 1, o.shape))
def setup_inputs_ends(rng):
    sh = (N, 8, 16, S); top = 2048 * NM
    z = 32 * 63 * rng.integers(0, 2, sh) + 15 * rng.integers(0, 2, sh) + 1
    e = np.where(rng.random(sh) < 0.28, 2048 * rng.integers(0, NM, sh) + z, top * rng.integers(0, 2, sh))
    k = rng.random((N, 8, 1, S)); last = 2048 * (NM - 1) + z
    e = np.where(k < 0.41, 16 + z, e); e = np.where(k < 0.37, z, e); e = np.where(k < 0.33, last, e)
    e = np.where(k < 0.26, 0, e); e = np.where(k < 0.16, top, e)
    x = 63 * (rng.random((N, 8, 16, NM)) < 0.2).astype(np.int64); x[..., NM - 1] = 63; x[..., 0] = 0
    w = at_ends(rng, 255); kp = at_ends(rng, 255); w[0, 7] = 255; w[N - 1, 7] = 255
    for c in [0, ST] + list(range(S - ST, S)): e[:, 7, :, c] = last[:, 7, :, c]
    u = 16 * 63 * 255 & 4095
    for m in (8, 15): e[0, 7, :, ((u * u >> 5) + int(kp[N - 1, 7, m]) * u) & (S - 1)] = top
    return done(e, x, w, kp)
def setup_inputs_corners(rng):
    nm, st, kd, ac, fu, x, w, kp = parts(rng, 6, 0.1); sh = kd.shape
    o = rng.permutation(8); md = o[(np.arange(8)[None, :] + (np.arange(N)[:, None] & 1)) & 7]; m4 = md[:, :, None, None]
    kd = np.where(m4 == 0, 1, np.where(m4 == 1, 0, kd)); fu = fu | (m4 == 1)
    fu = np.where(m4 == 2, rng.random((N, 8, 1, S)) < 0.5, fu)
    ac = np.where(m4 == 3, C0 - TAU - 1 + rng.integers(0, RO + 1, sh), ac); kd = np.where(m4 == 3, (rng.random(sh) < 0.7).astype(np.int64), kd)
    st = np.where(m4 == 4, 63 * rng.integers(0, 2, sh), st); st = np.where(m4 == 7, 31, st)
    kd = np.where(m4 == 6, ((np.arange(S)[None, :] & 15) != np.arange(16)[:, None]).astype(np.int64), kd); fu = fu | (m4 == 6)
    x = np.where(m4 == 5, 63, x); m3 = md[:, :, None]
    w = np.where(m3 == 4, 0, np.where(m3 == 7, 255, w)); kp = np.where(m3 == 6, 0, np.where(m3 == 7, 255, kp))
    return done(pack(nm, st, kd, ac, fu), x, w, kp)
def setup_inputs_ties(rng):
    nm, st, kd, ac, fu, x, w, kp = parts(rng, 3, 0.02); sh = st.shape
    st = rng.integers(0, 63, (1, 8, 16, 1)) + rng.integers(0, 2, sh)
    ac = rng.choice(np.array([0, C0 - TAU - 1, C0 - TAU, C0 - TAU + 1, C0, 15]), sh); fu = rng.random(sh) < 0.9
    e = pack(nm, st, kd, ac, fu)
    w[..., 0] |= 1; kp = np.argsort(rng.random((N, 8, 256)), axis=-1)[..., :16]
    nn = rng.integers(0, NM, (N, 8, 16)); c = np.zeros((N, 8, 16), np.int64)
    for r in range(N):
        for g in range(8):
            n = int(nn[r, g, 0])
            if int(np.add.reduce(w[r, g] * x[r, g, :, n])) & 1 == 0: x[r, g, 0, n] ^= 1
            u = int(np.add.reduce(w[r, g] * x[r, g, :, n])) & 4095
            c[r, g] = ((u * u >> 5) + kp[r, g] * u) & (S - 1)
    for r in range(N):
        for g in range(8):
            q = (r + 1) % N; l = min(i for i in range(17) if not np.any(c[r - 1, g] == ST * i))
            s = rng.integers(0, 64, 16); own = pack(nn[r, g], s, (np.arange(16) > 0).astype(np.int64), rng.integers(0, 16, 16), True)
            e[r, g, :, ST * l] = own
            d = rng.integers(1, 4, 16); m = np.sort(rng.permutation(16)[:2]); d[m] = np.array([1, 0]) if (r + g) & 1 else np.array([0, 1])
            miss = np.argsort(rng.random((16, 16)), axis=0) < d[None, :]
            hit = pack(nn[r, g][:, None], s[:, None] ^ rng.integers(1, 64, (16, 16)), rng.integers(0, 2, (16, 16)), rng.integers(0, 16, (16, 16)), True)
            no = np.where(rng.random((16, 16)) < 0.5, 0, (((own - 1) >> 4) << 4)[:, None] + 1 + rng.integers(0, 16, (16, 16)))
            e[q, g][:, c[r, g]] = np.where(miss, no, hit)
    return done(e, x, w, kp)
def gone(v, c):
    return np.where((((37 * c + v) >> 3) & 7) == 0, v ^ 8, v)
def setup_inputs_crowd(rng):
    nm, st, kd, ac, fu, x, w, kp = parts(rng, 8, 0.2)
    e = np.take_along_axis(pack(nm, st, kd, ac, fu), rng.integers(0, 24, (N, 8, 1, S)), 3)
    kp[:, ::2] = kp[:, ::2, :1]
    h = int(rng.integers(0, 8)); kp[:, h] = 0; w[:, h] = 0; w[:, h, 0] = 1; w[:, h, 15] = 64
    cols = ST * np.arange(1, L); sh = (16, L - 1)
    for r in range(N):
        q = (r + 1) % N; o = rng.permutation(4096); c = (o * o >> 5) & (S - 1)
        first = np.unique(c, return_index=True)[1]; first = first[c[first] % ST != 0]
        u = o[rng.permutation(first)[:L - 1]]; p = (u * u >> 5) & (S - 1)
        names = rng.permutation(NM)[:L - 1]; x[r, h, 0, names] = u & 63; x[r, h, 15, names] = u >> 6
        it = rng.random(sh) < 0.4; it[0] = True; it[15] = True
        a = pack(np.where(it, names[None, :], rng.integers(0, NM, sh)), rng.integers(0, 64, sh), 1 - it.astype(np.int64), rng.integers(0, C0 - TAU, sh), True)
        b = pack(gone(rng.integers(0, NM, sh), p[None, :]), rng.integers(0, 64, sh), 1, rng.integers(0, C0 - TAU, sh), True)
        full = rng.random(L - 1) < 0.5; full[-1] = True
        e[r, h][:, cols] = a
        e[q, h][:, p] = np.where(full[None, :], b, a)
    e[:, h, :, 0] = pack(gone(rng.integers(0, NM, 16), 0), rng.integers(0, 64, 16), 1, rng.integers(0, C0 - TAU, 16), True)[None, :]
    return done(e, x, w, kp)
def check_inputs(d):
    bad = []
    for k, lo, hi in (("ent", 0, 2048 * NM), ("feat", 0, 63), ("wt", 0, 255), ("kap", 0, 255)):
        v = np.asarray(d[k]).astype(np.float64)
        if not (np.min(v) >= lo and np.max(v) <= hi): bad.append("range of " + k)
        elif np.any(v != np.floor(v)): bad.append("whole numbers in " + k)
    return bad
def item(a):
    return (a > 0) & ((((a - 1) >> 4) & 1) == 0)
def asleep(a, clock):
    return (a > 0) & ((((a - 1) >> 4) & 1) == 1) & (clock - ((a - 1) & 15) > TAU)
def stay(a, site, clock):
    return np.where(asleep(a, clock) & ((((37 * site + ((a - 1) >> 11)) >> 3) & 7) != 0), 0, a)
def meet(a, b, clock):
    same = (a > 0) & (b > 0) & (((a - 1) >> 11) == ((b - 1) >> 11)); big = np.maximum(a, b)
    wake = same & asleep(big, clock) & item(np.minimum(a, b))
    big = np.where(wake, (((big - 1) >> 4) << 4) + clock + 1, big)
    return np.where(same, big, np.where((a == 0) & ~asleep(b, clock), b, a)), np.where(same, big, np.where((b == 0) & ~asleep(a, clock), a, b))
def reference(ent, feat, wt, kap):
    E = ent.astype(np.int64).reshape(N, 8, 16, S); X = feat.astype(np.float32).astype(np.int64).reshape(N, 8, 16, NM)
    w = wt.astype(np.int64).reshape(N, 8, 16, 1); kp = kap.astype(np.int64).reshape(N, 8, 16, 1); A = [0] * N
    for t in range(RO):
        clock = C0 + t; lane = ST * np.arange(L) + t % ST; new = E.copy(); called = []
        for r in range(N):
            q = (r + 1 + t % (N - 1)) % N
            a = E[r][:, :, lane]
            x = np.take_along_axis(X[r], np.maximum((a - 1) >> 11, 0).reshape(8, 1, 16 * L), 2).reshape(8, 16, 16, L)
            y = np.max(np.where(item(a)[:, None], x, 0), axis=2)
            u = np.add.reduce(w[r] * y, axis=1)[:, None, :] & 4095
            e = ((u * u >> 5) + kp[r] * u + A[r]) & (S - 1)
            cand = np.take_along_axis(E[q], e.reshape(8, 1, 16 * L), 2).reshape(8, 16, 16, L) - 1
            own = a[:, :, None, :] - 1
            score = np.add.reduce((((cand >> 11) == (own >> 11)) & ((cand >> 4) != (own >> 4))).astype(np.int64), axis=1)
            p = np.take_along_axis(e, np.argmax(score, axis=1)[:, None, :], 1)
            win = np.zeros((8, L), bool)
            for g in range(8): win[g, np.unique(p[g, 0], return_index=True)[1]] = True
            b = np.take_along_axis(E[q], p, 2)
            na, nb = meet(stay(a, lane[None, None, :], clock), stay(b, p, clock), clock)
            new[r][:, :, lane] = np.where(win[:, None, :], na, a)
            called.append((q, p[:, 0], win, nb)); A[r] = int(np.count_nonzero(win)) & 31
        for q, p, win, nb in called:
            for g in range(8): new[q, g][:, p[g, win[g]]] = nb[g][:, win[g]]
        E = new
    return {"yent": E.reshape(N, 128, S).astype(np.float32)}

@@ -1,0 +1,586 @@
+from concourse.bass import DstId, RemoteDMATransfer
+from concourse.mybir import dt, AluOpType, AxisListType, ActivationFunctionType
+
+N = 8
+RO = 4
+M0 = 12582912.0
+MB = M0 * 2048.0
+BIG = 1048576.0
+W = 2048 + 128
+NE = 8
+
+SCRATCH = {
+    "ents": ("sbuf", [128, 2048], "int32"),
+    "raw": ("sbuf", [128, W], "float32"),
+    "cod": ("sbuf", [128, W], "float32"),
+    "st": ("sbuf", [128, 2048], "float32"),
+    "fw": ("sbuf", [128, 4112], "bfloat16"),
+    "cf1": ("sbuf", [128, 2048], "float32"),
+    "cf2": ("sbuf", [128, 2048], "float32"),
+    "wti": ("sbuf", [128, 4], "int32"),
+    "kpi": ("sbuf", [128, 4], "int32"),
+    "ones": ("sbuf", [128, 160], "bfloat16"),
+    "one16": ("sbuf", [128, 128], "bfloat16"),
+    "bd0": ("sbuf", [128, 128], "bfloat16"),
+    "bd": ("sbuf", [128, 128], "bfloat16"),
+    "z0": ("sbuf", [128, 144], "bfloat16"),
+    "z1": ("sbuf", [128, 144], "bfloat16"),
+    "z2": ("sbuf", [128, 144], "bfloat16"),
+    "z": ("sbuf", [128, 144], "bfloat16"),
+    "iz": ("sbuf", [128, 160], "bfloat16"),
+    "iz0": ("sbuf", [128, 160], "float16"),
+    "iz1": ("sbuf", [128, 160], "float16"),
+    "sb": ("sbuf", [128, 128], "float16"),
+    "wblk": ("sbuf", [128, 128], "bfloat16"),
+    "fm": ("sbuf", [128, 2048], "bfloat16"),
+    "cli": ("sbuf", [128, 128], "int32"),
+    "cl": ("sbuf", [128, 128], "uint16"),
+    "pi": ("sbuf", [128, 4], "int32"),
+    "pcol": ("sbuf", [128, 16], "float32"),
+    "p16": ("sbuf", [128, 4], "int32"),
+    "ii": ("sbuf", [128, 8], "int32"),
+    "ij": ("sbuf", [128, 8], "int32"),
+    "dum": ("sbuf", [128, 8], "float32"),
+    "dmc": ("sbuf", [128, 8], "float32"),
+    "dl3": ("sbuf", [128, 32], "float32"),
+    "ji": ("sbuf", [128, 16], "int32"),
+    "tri": ("sbuf", [128, 8, 16], "bfloat16"),
+    "sti": ("sbuf", [128, 64], "int32"),
+    "stj": ("sbuf", [128, 64], "int32"),
+    "i1": ("sbuf", [128, 128], "int32"),
+    "i2": ("sbuf", [128, 128], "int32"),
+    "i3": ("sbuf", [128, 128], "int32"),
+    "f4": ("sbuf", [128, 128], "float32"),
+    "f5": ("sbuf", [128, 128], "float32"),
+    "lst": ("sbuf", [128, 128], "uint16"),
+    "fg": ("sbuf", [128, 2048], "bfloat16"),
+    "fs": ("sbuf", [128, 2048], "bfloat16"),
+    "u1": ("sbuf", [128, 128], "int32"),
+    "u2": ("sbuf", [128, 128], "int32"),
+    "u3": ("sbuf", [128, 128], "float32"),
+    "u4": ("sbuf", [128, 128], "float32"),
+    "u5": ("sbuf", [128, 128], "int32"),
+    "u6": ("sbuf", [128, 128], "int32"),
+    "se": ("sbuf", [128, 512], "uint16"),
+    "le": ("sbuf", [128, 512], "uint16"),
+    "so": ("sbuf", [128, 1024], "float32"),
+    "lo": ("sbuf", [128, 1024], "float32"),
+    "sa": ("sbuf", [128, 16], "float32"),
+    "la": ("sbuf", [128, 16], "float32"),
+    "sx": ("sbuf", [128, 4 * 392], "float32"),
+    "ln": ("sbuf", [128, 4 * 264], "float32"),
+    "ox": ("sbuf", [128, 2048], "float32"),
+    "dd": ("sbuf", [128, 2048], "bfloat16"),
+    "da": ("sbuf", [128, 2048], "bfloat16"),
+    "db": ("sbuf", [128, 2048], "bfloat16"),
+    "mt": ("sbuf", [128, 2048], "bfloat16"),
+    "eb": ("sbuf", [128, 128], "float32"),
+    "key": ("sbuf", [128, 128], "float32"),
+    "kt": ("sbuf", [128, 128], "float32"),
+    "ks": ("sbuf", [128, 128], "float32"),
+    "kr": ("sbuf", [128, 128], "float32"),
+    "et": ("sbuf", [128, 128], "float16"),
+    "rt": ("sbuf", [128, 128], "float16"),
+    "row": ("sbuf", [128, 128], "float16"),
+    "eq": ("sbuf", [128, 8, 144], "bfloat16"),
+    "l1": ("sbuf", [128, 8], "uint16"),
+    "l2": ("sbuf", [128, 32], "uint16"),
+    "l3": ("sbuf", [128, 32], "uint16"),
+    "dl2": ("sbuf", [128, 8], "float32"),
+    "w2": ("sbuf", [128, 8], "float32"),
+    "w2b": ("sbuf", [128, 8], "float32"),
+    "w3": ("sbuf", [128, 8], "float32"),
+    "win": ("sbuf", [128, 128], "bfloat16"),
+    "wj": ("sbuf", [128, 128], "bfloat16"),
+    "cab": ("sbuf", [128, 4], "bfloat16"),
+    "ah": ("sbuf", [128, 128], "int32"),
+    "al": ("sbuf", [128, 128], "int32"),
+    "ak": ("sbuf", [128, 128], "int32"),
+    "an": ("sbuf", [128, 128], "float32"),
+    "av": ("sbuf", [128, 128], "float32"),
+    "aq": ("sbuf", [128, 128], "float32"),
+    "am": ("sbuf", [128, 128], "float32"),
+    "ti": ("sbuf", [128, 128], "float32"),
+    "ea": ("sbuf", [128, 128], "float32"),
+    "ef": ("sbuf", [128, 128], "float32"),
+    "c0": ("sbuf", [128, 128], "float32"),
+    "c1": ("sbuf", [128, 128], "float32"),
+    "bg": ("sbuf", [128, 128], "float32"),
+    "bh": ("sbuf", [128, 128], "int32"),
+    "bl": ("sbuf", [128, 128], "int32"),
+    "bk": ("sbuf", [128, 128], "int32"),
+    "bn": ("sbuf", [128, 128], "float32"),
+    "bv": ("sbuf", [128, 128], "float32"),
+    "bp": ("sbuf", [128, 128], "float32"),
+    "gb": ("sbuf", [128, 128], "float32"),
+    "di": ("sbuf", [128, 128], "float32"),
+    "dq": ("sbuf", [128, 128], "float32"),
+    "sm": ("sbuf", [128, 128], "float32"),
+    "t1": ("sbuf", [128, 128], "float32"),
+    "t1b": ("sbuf", [128, 128], "float32"),
+    "t1c": ("sbuf", [128, 128], "float32"),
+    "bq": ("sbuf", [128, 128], "float32"),
+    "bm": ("sbuf", [128, 128], "float32"),
+    "t2": ("sbuf", [128, 128], "float32"),
+    "t2b": ("sbuf", [128, 128], "float32"),
+    "mx": ("sbuf", [128, 128], "float32"),
+    "pp": ("sbuf", [128, 128], "float32"),
+    "x1": ("sbuf", [128, 256], "float32"),
+    "x2": ("sbuf", [128, 256], "float32"),
+    "ebz": ("sbuf", [128, 128], "float32"),
+    "nbc": ("sbuf", [128, 512], "float32"),
+    "psU": ("psum", [128, 512], "float32"),
+    "psK0": ("psum", [128, 512], "float32"),
+    "psK1": ("psum", [128, 512], "float32"),
+    "psL": ("psum", [128, 512], "float32"),
+    "psR": ("psum", [128, 512], "float32"),
+    "psC": ("psum", [128, 512], "float32"),
+    "psG": ("psum", [128, 512], "float32"),
+    "psV": ("psum", [128, 512], "float32"),
+}
+SEMAPHORES = (["sV", "sA", "sP", "sG", "dent", "dsm", "dfe", "dst", "dy", "loc"]
+              + ["ro%d" % t for t in range(RO)] + ["re%d%d" % (t, h) for t in range(RO) for h in range(2)]
+              + ["rn%d" % t for t in range(RO)] + ["ra%d" % t for t in range(RO)])
+
+
+def rank_program(g, core, T, topo):
+    rank = T.rank_of(core)
+    if rank is None:
+        return
+    A = AluOpType
+    F = ActivationFunctionType
+    Q = {"V": g.vector, "A": g.scalar, "P": g.tensor, "G": g, "S": g.sync}
+    tot = {}
+    seen = {"V": {}, "A": {}, "P": {}, "G": {}, "S": {}}
+    wr, rd = {}, {}
+    v, a, pe = g.vector, g.scalar, g.tensor
+
+    def wait(q, evs):
+        evs = [e for e in evs if seen[q].get(e[0], 0) < e[1]]
+        for i, e in enumerate(evs):
+            if seen[q].get(e[0], 0) >= e[1]:
+                continue
+            if any(o is not e and o[2].get(e[0], 0) >= e[1] for o in evs):
+                continue
+            Q[q].wait_ge(T.sem[e[0]], e[1])
+            seen[q][e[0]] = e[1]
+        for e in evs:
+            for s, n in e[2].items():
+                if seen[q].get(s, 0) < n:
+                    seen[q][s] = n
+
+    def deps(q, r, w, dma):
+        evs = []
+        for k in r:
+            evs += [e for o, e in wr.get(k, [])]
+            if k[:2] == "ps":
+                evs += [e for o, e in rd.get(k, []) if o != q]
+        for k in w:
+            evs += [e for o, e in wr.get(k, []) if not (q == "P" and o == "P")]
+            evs += [e for o, e in rd.get(k, []) if dma or o != q]
+        return evs
+
+    def note(q, r, w, ev):
+        for k in w:
+            if q == "P" and wr.get(k) and wr[k][0][0] == "P":
+                wr[k] = [(q, ev)]
+            else:
+                wr[k] = [(q, ev)]
+            rd[k] = []
+        for k in r:
+            rd[k] = [x for x in rd.get(k, []) if x[0] != q or q == "D"] + [(q, ev)]
+
+    def op(q, fn, r, w, x=()):
+        wait(q, deps(q, r, w, False) + list(x))
+        s = "s" + q
+        tot[s] = tot.get(s, 0) + 1
+        fn().then_inc(T.sem[s], 1)
+        clk = dict(seen[q])
+        clk[s] = tot[s]
+        note(q, r, w, (s, tot[s], clk))
+
+    def dma(q, out, in_, r, w, s):
+        wait(q, deps(q, r, w, True))
+        Q[q].dma_start(out, in_).then_inc(T.sem[s], 16)
+        tot[s] = tot.get(s, 0) + 16
+        clk = dict(seen[q])
+        clk[s] = tot[s]
+        note("D", r, w, (s, tot[s], clk))
+
+    def joined(k, s):
+        wr[k] = [("D", (s, tot[s], {s: tot[s]}))]
+
+    def send(dst, out, in_, r, s):
+        wait("G", deps("G", r, [], True))
+        rid, pid = topo.addr(dst)[:2]
+        m = 0
+        for e in topo.engines(core, dst)[:NE]:
+            m |= 1 << e
+        g.remote_dma(out, in_, T.sem[s], T.sem["loc"], pid, rid, m)
+        tot["loc"] = tot.get("loc", 0) + NE
+
+    def landed(k, s):
+        tot[s] = NE
+        wr[k] = [("R", (s, NE, {s: NE}))]
+
+    def ts(out, in0, s1, s2, o0, o1, r, w):
+        if o1 is None:
+            op("V", lambda: v.tensor_scalar(out, in0, s1, None, o0), r, w)
+        else:
+            op("V", lambda: v.tensor_scalar(out, in0, s1, s2, o0, o1), r, w)
+
+    def tt(out, i0, i1, o, r, w):
+        op("V", lambda: v.tensor_tensor(out, i0, i1, o), r, w)
+
+    def vc(out, in_, r, w):
+        op("V", lambda: v.tensor_copy(out, in_), r, w)
+
+    def act(out, in_, f, r, w, bias=0.0, scale=1.0):
+        op("A", lambda: a.activation(out, in_, f, bias=bias, scale=scale), r, w)
+
+    def mm(out, l, rh, st, sp, r, w):
+        op("P", lambda: pe.matmul(out, l, rh, st, sp), r, w)
+
+    def ms(ap, c, w):
+        op("V", lambda: v.memset(ap, c), [], w)
+
+    dma("S", T.ents[:, 0:1024], T.ent[:, 0:1024], [], ["ents"], "dent")
+    dma("A", T.ents[:, 1024:2048], T.ent[:, 1024:2048], [], [], "dent")
+    joined("ents", "dent")
+    dma("S", T.fw[:, 0:2048], T.feat[:, 0:2048], [], [], "dfe")
+    dma("A", T.fw[:, 2048:4096], T.feat[:, 2048:4096], [], [], "dfe")
+    joined("fw", "dfe")
+    dma("S", T.wti[:, 0:1], T.wt[:, 0:1], [], [], "dsm")
+    dma("S", T.kpi[:, 0:1], T.kap[:, 0:1], [], [], "dsm")
+    joined("wti", "dsm")
+    joined("kpi", "dsm")
+
+    ms(T.ones[:], 1.0, ["ones"])
+    op("G", lambda: g.iota(T.pi[:, 0:1], [[1, 1]], 0, 1), [], ["pi"])
+    op("G", lambda: g.iota(T.cli[:], [[1, 128]], 0, 0), [], ["cli"])
+    op("G", lambda: g.iota(T.sti[:], [[37, 64]], 0, 0), [], ["sti"])
+    op("G", lambda: g.affine_select(T.bd0[:], T.ones[:, 0:128], [[-16, 8], [0, 16]], A.is_ge, 0.0, 0, 1), ["ones"], ["bd0"])
+    op("G", lambda: g.affine_select(T.bd[:], T.bd0[:], [[16, 8], [0, 16]], A.is_ge, 0.0, 15, -1), ["bd0"], ["bd"])
+    op("G", lambda: g.iota(T.ii[:], [[16, 8]], 2048, 0), [], ["ii"])
+    op("G", lambda: g.iota(T.ij[:], [[256, 8]], 0, 0), [], ["ij"])
+    op("G", lambda: g.iota(T.ji[:], [[1, 16]], 0, 0), [], ["ji"])
+    op("G", lambda: g.affine_select(T.z0[:], T.ones[:, 0:144], [[-16, 9], [0, 16]], A.is_ge, 0.0, 0, 1), ["ones"], ["z0"])
+    op("G", lambda: g.affine_select(T.z1[:], T.z0[:], [[16, 9], [0, 16]], A.is_ge, 0.0, 15, -1), ["z0"], ["z1"])
+    op("G", lambda: g.affine_select(T.z2[:], T.z1[:], [[0, 9], [1, 16]], A.is_equal, 0.0, -15, 0), ["z1"], ["z2"])
+    op("G", lambda: g.affine_select(T.iz[:], T.ones[:], [[-1, 160]], A.is_equal, 0.0, 16, 1), ["ones"], ["iz"])
+    ms(T.fw[:, 4096:4112], 0.0, ["fwz"])
+    ms(T.fm[:], 1.0, ["fm"])
+    ms(T.fm[:, 0:2048:16], 0.0, ["fm"])
+    ms(T.one16[:], 0.0625, ["one16"])
+    ms(T.pcol[:, 8:9], -0.375, ["acol"])
+    ms(T.sa[:], 0.0, ["sa"])
+    ts(T.p16[:, 0:1], T.pi[:, 0:1], 15, None, A.bitwise_and, None, ["pi"], ["p16"])
+    ts(T.p16[:, 1:2], T.pi[:, 0:1], 16, None, A.bitwise_and, None, ["pi"], ["p16b"])
+    vc(T.pcol[:, 0:1], T.p16[:, 0:1], ["p16"], ["pc0"])
+    ts(T.pcol[:, 1:2], T.p16[:, 1:2], 0.0, None, A.is_equal, None, ["p16b"], ["pc1"])
+    ts(T.pcol[:, 2:3], T.p16[:, 1:2], 0.0, None, A.is_gt, None, ["p16b"], ["pc2"])
+    ts(T.pcol[:, 3:4], T.p16[:, 0:1], -2048.0, 15 * 2048 - 1023.5, A.mult, A.add, ["p16"], ["pc3"])
+    ts(T.pcol[:, 4:5], T.p16[:, 0:1], 15.0, None, A.is_equal, None, ["p16"], ["pc4"])
+    ts(T.pcol[:, 5:6], T.p16[:, 0:1], 16.0, None, A.mult, None, ["p16"], ["pc5"])
+    vc(T.cl[:], T.cli[:], ["cli"], ["cl"])
+    ts(T.stj[:], T.sti[:], 63, None, A.bitwise_and, None, ["sti"], ["stj"])
+    ts(T.st[:, 0:64], T.stj[:], 2048.0, -17.0, A.mult, A.add, ["stj"], ["st"])
+    ts(T.dum[:], T.ii[:], T.pcol[:, 0:1], None, A.add, None, ["ii", "pc0"], ["dum"])
+    ts(T.dmc[:], T.dum[:], -1023.5, None, A.add, None, ["dum"], ["dmc"])
+    ts(T.w3[:], T.ij[:], T.pcol[:, 5:6], None, A.add, None, ["ij", "pc5"], ["w3"])
+    tt(T.w2[:], T.w3[:], T.dum[:], A.subtract, ["w3", "dum"], ["w2"])
+    for t in range(RO):
+        ts(T.dl3[:, 8 * t:8 * t + 8], T.w2[:], float(t), None, A.add, None, ["w2"], ["dl3"])
+    for c in range(8):
+        ts(T.tri[:, c, 0:16], T.ji[:], T.pcol[:, 0:1], None, A.is_gt, None, ["ji", "pc0"], ["tri"])
+    n = 64
+    while n < 2048:
+        dma("S", T.st[:, n:2 * n], T.st[:, 0:n], ["st"], ["st"], "dst")
+        n *= 2
+
+    def first_table():
+        banks = ["psK0", "psK1", "psR", "psC"]
+        for i in range(4):
+            s = slice(512 * i, 512 * i + 512)
+            k = "@%d" % i
+            vc(T.raw[:, s], T.ents[:, s], ["ents"], ["raw" + k])
+            ts(T.cf1[:, s], T.ents[:, s], -1024.5, MB, A.add, A.add, ["ents"], ["cf1" + k])
+            act(T.cf2[:, s], T.raw[:, s], F.Identity, ["raw" + k], ["cf2" + k], bias=T.bcol[:, 0:1])
+            act(T[banks[i]][:], T.cf1[:, s], F.Identity, ["cf1" + k], [banks[i]], bias=T.bcol[:, 1:2], scale=0.0625)
+            act(T.cf2[:, s], T.cf2[:, s], F.Identity, ["cf2" + k], ["cf2" + k], bias=T.bcol[:, 2:3], scale=0.0625)
+        for i in range(4):
+            s = slice(512 * i, 512 * i + 512)
+            k = "@%d" % i
+            tt(T.cod[:, s], T[banks[i]][:], T.cf2[:, s], A.add, [banks[i], "cf2" + k], ["code"] if i == 3 else [])
+            wr["code"] = wr.get("code", [])
+        wr["raw"] = list(wr["raw@3"])
+
+    ms(T.bcol[:, 0:1], -8.5, ["bc0"])
+    ms(T.bcol[:, 1:2], -MB / 16, ["bc1"])
+    ms(T.bcol[:, 2:3], M0, ["bc2"])
+    ms(T.bcol[:, 3:4], -64.0, ["bc3"])
+    wait("A", [wr[k][0][1] for k in ("bc0", "bc1", "bc2", "bc3")])
+
+    VS = 24
+    WC = 4112
+    keys = {"lists": ["fw", "fwz"]}
+
+    def lane_list(t):
+        src, sk = (T.ents, "ents") if t == 0 else (T.raw, "raw")
+        ts(T.i1[:], src[:, t:2048:16], -1.0, None, A.add, None, [sk], ["i1"])
+        ts(T.i2[:], T.i1[:], 11, None, A.arith_shift_right, None, ["i1"], ["i2"])
+        ts(T.i3[:], T.i1[:], 16, None, A.bitwise_and, None, ["i1"], ["i3"])
+        ts(T.f4[:], T.i3[:], 512.0, None, A.mult, None, ["i3"], ["f4"])
+        tt(T.f5[:], T.i2[:], T.f4[:], A.add, ["i2", "f4"], ["f5"])
+        ts(T.lst[:], T.f5[:], 4096.0, None, A.min, None, ["f5"], ["lst"])
+
+    def feat_act(h):
+        l0, l1 = 64 * h + VS, 64 * h + 64
+        op("A", lambda: a.activation(T.fg[:, 16 * l0:16 * l1], T.fw[:, 0:WC].indirect(T.lst[:, l0:l1]), F.Copy),
+           ["lst"] + keys["lists"], ["fgA%d" % h])
+
+    def feat_vec(h):
+        l0, l1 = 64 * h, 64 * h + VS
+        op("V", lambda: v.tensor_copy(T.fg[:, 16 * l0:16 * l1], T.fw[:, 0:WC].indirect(T.lst[:, l0:l1])),
+           ["lst"] + keys["lists"], ["fgV%d" % h])
+        for n0, n1, k in ((l0, l1, "V"), (l1, 64 * h + 64, "A")):
+            c = slice(16 * n0, 16 * n1)
+            op("V", lambda: v.tensor_tensor_scan(T.fs[:, c], T.fm[:, c], T.fg[:, c], 0.0, A.mult, A.max),
+               ["fm", "fg%s%d" % (k, h)], ["fs%d" % h])
+        mm(T.psU[:, 64 * h:64 * h + 64], T.wblk[:], T.fs[:, 1024 * h + 15:1024 * h + 1024:16], True, True,
+           ["wblk", "fs%d" % h], ["psU"])
+
+    def cand(t, h, dst):
+        s = slice(64 * h, 64 * h + 64)
+        o = 128 * t + 64 * h
+        ac = T.pcol[:, 8:9] if t == 0 else T.la[:, 4 * t - 4:4 * t - 3]
+        vc(T.u1[:, s], T.psU[:, s], ["psU"], ["u1"])
+        ts(T.u2[:, s], T.u1[:, s], 4095, None, A.bitwise_and, None, ["u1"], ["u2"])
+        ts(T.u3[:, s], T.u2[:, s], 0.03125, T.pcol[:, 7:8], A.mult, A.add, ["u2", "kcol"], ["u3"])
+        tt(T.u4[:, s], T.u3[:, s], T.u2[:, s], A.mult, ["u3", "u2"], ["u4"])
+        ts(T.u5[:, s], T.u4[:, s], ac, None, A.add, None, ["u4", "acol" if t == 0 else "la%d" % (t - 1)], ["u5"])
+        ts(T.u6[:, s], T.u5[:, s], 2047, None, A.bitwise_and, None, ["u5"], ["u6"])
+        vc(T.se[:, o:o + 64], T.u6[:, s], ["u6"], ["se%d%d" % (t, h)])
+        send(dst, T.le[:, o:o + 64], T.se[:, o:o + 64], ["se%d%d" % (t, h)], "re%d%d" % (t, h))
+
+    def own_send(t, dst):
+        o = 256 * t
+        act(T.so[:, o:o + 128], T.raw[:, t:2048:16], F.Copy, ["raw"], ["so%da" % t])
+        act(T.so[:, o + 128:o + 256], T.cod[:, t:2048:16], F.Copy, ["code"], ["so%db" % t])
+        send(dst, T.lo[:, o:o + 256], T.so[:, o:o + 256], ["so%da" % t, "so%db" % t], "ro%d" % t)
+
+    def scatter(tab, lists, vals, r, w):
+        op("V", lambda: v.tensor_copy(T[tab][:, 0:W].indirect(lists), vals), r, w)
+
+    def own_side(t):
+        o = 256 * t
+        th, ck = 8.0 + t, 12.0 + t
+        av, lk = T.lo[:, o:o + 128], "lo%d" % t
+        tt(T.ah[:], av, T.st[:, t:2048:16], A.add, [lk, "st"], ["ah"])
+        ts(T.al[:], T.ah[:], 31, None, A.bitwise_and, None, ["ah"], ["al"])
+        ts(T.ak[:], T.ah[:], 114688, None, A.bitwise_and, None, ["ah"], ["ak"])
+        ts(T.an[:], T.al[:], th, BIG, A.is_ge, A.mult, ["al"], ["an"])
+        tt(T.av[:], T.ak[:], T.an[:], A.is_le, ["ak", "an"], ["av"])
+        tt(T.psV[:, 0:128], av, T.av[:], A.mult, [lk, "av"], ["psV"])
+        ts(T.aq[:], T.al[:], -1.0, ck, A.mult, A.add, ["al"], ["aq"])
+        ts(T.am[:], T.al[:], th, None, A.is_lt, None, ["al"], ["am"])
+        ts(T.ea[:], T.psV[:, 0:128], 0.0, 1.0 / BIG, A.is_equal, A.mult, ["psV"], ["ea"])
+        ts(T.ef[:], T.psV[:, 0:128], 0.0, -16.0 * BIG, A.is_equal, A.mult, ["psV"], ["ef"])
+        ts(T.c0[:], av, -1024.5, MB, A.add, A.add, [lk], ["c0"])
+        ts(T.c1[:], T.c0[:], -MB, 1024.5, A.add, A.add, ["c0"], ["c1"])
+        ts(T.ti[:], T.al[:], 16.0, th, A.is_ge, A.mult, ["al"], ["ti"])
+        tt(T.psV[:, 128:256], T.aq[:], T.am[:], A.mult, ["aq", "am"], ["psV"])
+        tt(T.psV[:, 256:384], T.c1[:], T.ef[:], A.add, ["c1", "ef"], ["psV"])
+        tt(T.psV[:, 384:512], av, T.an[:], A.mult, [lk, "an"], ["psV"])
+
+    def expand(t, h):
+        o = 256 * t + 128
+        op("A", lambda: a.activation(T.ox[:, 1024 * h:1024 * h + 1024],
+                                     T.lo[:, o:o + 128].indirect(T.cl[:, 64 * h:64 * h + 64]), F.Copy),
+           ["lo%d" % t, "cl"], ["ox%d" % h])
+
+    def score(t):
+        def gat(i):
+            c = slice(512 * i, 512 * i + 512)
+            o = 128 * t + 32 * i
+            op("V", lambda: v.tensor_tensor(T.dd[:, c], T.cod[:, 0:2048].indirect(T.le[:, o:o + 32]), T.ox[:, c], A.subtract),
+               ["code", "le%d%d" % (t, i // 2), "ox%d" % (i // 2)], ["dd%d" % i])
+            act(T.da[:, c], T.dd[:, c], F.Abs, ["dd%d" % i], ["da%d" % i])
+            act(T.db[:, c], T.da[:, c], F.Abs, ["da%d" % i], ["db%d" % i], bias=T.bcol[:, 3:4])
+
+        def thr(i):
+            c = slice(512 * i, 512 * i + 512)
+            ts(T.mt[:, c], T.db[:, c], 63.75, None, A.is_lt, None, ["db%d" % i], ["mt%d" % i])
+
+        def add(h):
+            k = "psK%d" % h
+            for m in range(16):
+                mm(T[k][:, 0:64], T.z[:, 15 - m:143 - m], T.mt[:, 1024 * h + m:1024 * h + 1024:16], m == 0, m == 15,
+                   ["z", "mt%d" % (2 * h), "mt%d" % (2 * h + 1)], [k])
+
+        def keyh(h):
+            s = slice(64 * h, 64 * h + 64)
+            tt(T.key[:, s], T["psK%d" % h][:, 0:64], T.eb[:, s], A.add, ["psK%d" % h, "eb%d" % h], ["key%d" % h])
+
+        for h in range(2):
+            s = slice(64 * h, 64 * h + 64)
+            o = 128 * t + 64 * h
+            ts(T.eb[:, s], T.le[:, o:o + 64], T.pcol[:, 3:4], None, A.add, None, ["le%d%d" % (t, h), "pc3"], ["eb%d" % h])
+            gat(2 * h)
+            if h:
+                thr(1)
+                add(0)
+            gat(2 * h + 1)
+            thr(2 * h)
+        keyh(0)
+        thr(3)
+        add(1)
+        keyh(1)
+
+    def partner(t):
+        op("V", lambda: v.transpose(T.kt[:], T.key[:]), ["key0", "key1"], ["kt"])
+        op("V", lambda: v.tensor_tensor_scan(T.ks[:], T.fm[:, 0:128], T.kt[:], 0.0, A.mult, A.max), ["fm", "kt"], ["ks"])
+        ts(T.kr[:], T.ks[:], MB, -MB, A.add, A.add, ["ks"], ["kr"])
+        tt(T.et[:], T.ks[:], T.kr[:], A.subtract, ["ks", "kr"], ["et"])
+        for h in range(2):
+            for g2 in range(2):
+                b = 16 - 16 * (g2 - h)
+                mm(T.psL[:, h:8:2], T["iz%d" % h][:, b:b + 128], T.et[:, 16 * g2 + 15:128:32], g2 == 0, g2 == 1,
+                   ["iz%d" % h, "et"], ["psL"])
+        op("V", lambda: v.transpose(T.rt[:], T.et[:]), ["et"], ["rt"])
+        mm(T.psR[:, 0:128], T.sb[:], T.rt[:], True, True, ["sb", "rt"], ["psR"])
+        ts(T.l1[:], T.psL[:, 0:8], 1023.5, None, A.add, None, ["psL"], ["l1"])
+        vc(T.row[:], T.psR[:, 0:128], ["psR"], ["row"])
+        for c in range(8):
+            op("V", lambda: v.tensor_scalar(T.eq[:, c, 0:128 - 16 * c], T.row[:, 16 * c:128], T.psL[:, c:c + 1], None, A.is_equal),
+               ["row", "psL"], ["eq"])
+        tt(T.eq[:, :, 0:16], T.eq[:, :, 0:16], T.tri[:], A.mult, ["eq", "tri"], ["eq"])
+        for c in range(8):
+            mm(T.psC[:, 16 * c:128], T.bd[:], T.eq[:, c, 0:128 - 16 * c], c == 0, c == 7, ["bd", "eq"], ["psC"])
+        op("V", lambda: v.tensor_copy(T.bg[:], T.raw[:, 0:2048].indirect(T.l1[:])), ["raw", "l1"], ["bg"])
+        op("V", lambda: v.tensor_tensor(T.bh[:], T.st[:, 0:2048].indirect(T.l1[:]), T.bg[:], A.add), ["st", "l1", "bg"], ["bh"])
+        tt(T.dl2[:], T.psL[:, 0:8], T.dmc[:], A.subtract, ["psL", "dmc"], ["dl2"])
+        ts(T.win[:], T.psC[:, 0:128], 0.5, 2.0 ** -19, A.is_lt, A.mult, ["psC"], ["win"])
+        for s in range(16):
+            mm(T.psC[:, 128:136], T.z[:, 15 - s:143 - s], T.win[:, s:128:16], s == 0, s == 15, ["z", "win"], ["psC"])
+        if t < RO - 1:
+            op("A", lambda: a.activation(T.wj[:], T.win[:], F.Copy, scale=2.0 ** 19, accum_out=T.pcol[:, 9:10]), ["win"], ["wj", "ca"])
+            act(T.cab[:, 0:1], T.pcol[:, 9:10], F.Copy, ["ca"], ["cab"])
+            mm(T.psC[:, 136:137], T.one16[:], T.cab[:, 0:1], True, True, ["one16", "cab"], ["psC"])
+
+    def meet(t, dst):
+        th, ck = 8.0 + t, 12.0 + t
+        X = 392 * t
+        ts(T.bl[:], T.bh[:], 31, None, A.bitwise_and, None, ["bh"], ["bl"])
+        ts(T.bk[:], T.bh[:], 114688, None, A.bitwise_and, None, ["bh"], ["bk"])
+        ts(T.bn[:], T.bl[:], th, BIG, A.is_ge, A.mult, ["bl"], ["bn"])
+        tt(T.bv[:], T.bk[:], T.bn[:], A.is_le, ["bk", "bn"], ["bv"])
+        tt(T.bp[:], T.bg[:], T.bv[:], A.mult, ["bg", "bv"], ["bp"])
+        tt(T.di[:], T.bp[:], T.psV[:, 256:384], A.subtract, ["bp", "psV"], ["di"])
+        act(T.dq[:], T.di[:], F.Square, ["di"], ["dq"], scale=1.0 / 1024)
+        if t < RO - 1:
+            vc(T.p16[:, 2:3], T.psC[:, 136:137], ["psC"], ["ai"])
+            ts(T.p16[:, 3:4], T.p16[:, 2:3], 31, None, A.bitwise_and, None, ["ai"], ["aj"])
+            ts(T.sa[:, 4 * t:4 * t + 1], T.p16[:, 3:4], -0.375, None, A.add, None, ["aj"], ["sa%d" % t])
+            send(dst, T.la[:, 4 * t:4 * t + 4], T.sa[:, 4 * t:4 * t + 4], ["sa", "sa%d" % t], "ra%d" % t)
+        tt(T.gb[:], T.bg[:], T.bn[:], A.mult, ["bg", "bn"], ["gb"])
+        ts(T.t1[:], T.bl[:], 16.0, None, A.is_ge, None, ["bl"], ["t1"])
+        ts(T.bq[:], T.bl[:], -1.0, ck, A.mult, A.add, ["bl"], ["bq"])
+        tt(T.bm[:], T.bl[:], T.ti[:], A.is_lt, ["bl", "ti"], ["bm"])
+        tt(T.t1b[:], T.t1[:], T.psV[:, 128:256], A.mult, ["t1", "psV"], ["t1b"])
+        tt(T.t2[:], T.bq[:], T.bm[:], A.mult, ["bq", "bm"], ["t2"])
+        tt(T.t1c[:], T.t1b[:], T.psV[:, 0:128], A.add, ["t1b", "psV"], ["t1c"])
+        tt(T.t2b[:], T.t2[:], T.bp[:], A.add, ["t2", "bp"], ["t2b"])
+        ts(T.ebz[:], T.bp[:], 0.0, 1.0 / BIG, A.is_equal, A.mult, ["bp"], ["ebz"])
+        tt(T.mx[:], T.t1c[:], T.t2b[:], A.max, ["t1c", "t2b"], ["mx"])
+        tt(T.x2[:, 0:128], T.ebz[:], T.psV[:, 384:512], A.mult, ["ebz", "psV"], ["x2"])
+        ts(T.sm[:], T.dq[:], 1.0, None, A.is_lt, None, ["dq"], ["sm"])
+        tt(T.x2[:, 128:256], T.x2[:, 0:128], T.bp[:], A.max, ["x2", "bp"], ["x2b"])
+        tt(T.pp[:], T.sm[:], T.mx[:], A.mult, ["sm", "mx"], ["pp"])
+        tt(T.w2[:], T.psC[:, 128:136], T.dl2[:], A.mult, ["psC", "dl2"], ["w2"])
+        tt(T.sx[:, X:X + 128], T.x2[:, 128:256], T.pp[:], A.max, ["x2b", "pp"], ["nb%d" % t])
+        tt(T.w2b[:], T.w2[:], T.dum[:], A.add, ["w2", "dum"], ["w2b"])
+        tt(T.x1[:, 0:128], T.gb[:], T.ea[:], A.mult, ["gb", "ea"], ["x1"])
+        vc(T.l2[:, 8 * t:8 * t + 8], T.w2b[:], ["w2b"], ["l2%d" % t])
+        if t < RO - 1:
+            scatter("raw", T.l2[:, 8 * t:8 * t + 8], T.sx[:, X:X + 128], ["l2%d" % t, "nb%d" % t], ["raw"])
+        tt(T.x1[:, 128:256], T.x1[:, 0:128], T.psV[:, 0:128], A.max, ["x1", "psV"], ["x1b"])
+        tt(T.w3[:], T.psC[:, 128:136], T.dl3[:, 8 * t:8 * t + 8], A.mult, ["psC", "dl3"], ["w3"])
+        tt(T.sx[:, X + 128:X + 256], T.x1[:, 128:256], T.pp[:], A.max, ["x1b", "pp"], ["na%d" % t])
+        o = X + 384 if t < RO - 1 else X + 256
+        tt(T.sx[:, o:o + 8], T.w3[:], T.dum[:], A.add, ["w3", "dum"], ["nl%d" % t])
+        if t == RO - 1:
+            send(dst, T.ln[:, 264 * t:264 * t + 136], T.sx[:, X + 128:X + 264], ["na%d" % t, "nl%d" % t], "rn%d" % t)
+            return
+        z = slice(X, X + 256)
+        ts(T.cf1[:, 0:256], T.sx[:, z], -1024.5, MB, A.add, A.add, ["nb%d" % t, "na%d" % t], ["cf1"])
+        act(T.cf2[:, 0:256], T.sx[:, z], F.Identity, ["nb%d" % t, "na%d" % t], ["cf2"], bias=T.bcol[:, 0:1])
+        act(T.psG[:, 0:256], T.cf1[:, 0:256], F.Identity, ["cf1"], ["psG"], bias=T.bcol[:, 1:2], scale=0.0625)
+        act(T.cf2[:, 0:256], T.cf2[:, 0:256], F.Identity, ["cf2"], ["cf2"], bias=T.bcol[:, 2:3], scale=0.0625)
+
+    def finish(t, dst):
+        X = 392 * t
+        tt(T.nbc[:, 128 * t:128 * t + 128], T.psG[:, 0:128], T.cf2[:, 0:128], A.add, ["psG", "cf2"], ["nbc%d" % t])
+        tt(T.sx[:, X + 256:X + 384], T.psG[:, 128:256], T.cf2[:, 128:256], A.add, ["psG", "cf2"], ["nc%d" % t])
+        scatter("cod", T.l2[:, 8 * t:8 * t + 8], T.nbc[:, 128 * t:128 * t + 128], ["l2%d" % t, "nbc%d" % t], ["code"])
+        send(dst, T.ln[:, 264 * t:264 * t + 264], T.sx[:, X + 128:X + 392], ["na%d" % t, "nc%d" % t, "nl%d" % t], "rn%d" % t)
+
+    def back(t):
+        o = 264 * t
+        X = 392 * t
+        last = t == RO - 1
+        lo = o + (128 if last else 256)
+        lk = "ln%d" % t
+        l3, l2 = T.l3[:, 8 * t:8 * t + 8], T.l2[:, 8 * t:8 * t + 8]
+        vc(l3, T.ln[:, lo:lo + 8], [lk], ["l3%d" % t])
+        scatter("raw", l3, T.ln[:, o:o + 128], [lk, "l3%d" % t], ["raw"])
+        if not last:
+            scatter("cod", l3, T.ln[:, o + 128:o + 256], [lk, "l3%d" % t], ["code"])
+            scatter("cod", l2, T.nbc[:, 128 * t:128 * t + 128], ["l2%d" % t, "nbc%d" % t], ["code"])
+        scatter("raw", l2, T.sx[:, X:X + 128], ["l2%d" % t, "nb%d" % t], ["raw"])
+
+    for t in range(RO):
+        callee = T.cores[(rank + 1 + t % 7) % N]
+        caller = T.cores[(rank - 1 - t % 7) % N]
+        landed("lo%d" % t, "ro%d" % t)
+        landed("le%d0" % t, "re%d0" % t)
+        landed("le%d1" % t, "re%d1" % t)
+        landed("ln%d" % t, "rn%d" % t)
+        if t < RO - 1:
+            landed("la%d" % t, "ra%d" % t)
+        lane_list(t)
+        if t == 0:
+            vc(T.pcol[:, 6:7], T.wti[:, 0:1], ["wti"], ["wcol"])
+            vc(T.pcol[:, 7:8], T.kpi[:, 0:1], ["kpi"], ["kcol"])
+            ts(T.wblk[:], T.bd[:], T.pcol[:, 6:7], None, A.mult, None, ["bd", "wcol"], ["wblk"])
+            first_table()
+            ts(T.z[:], T.z2[:], 32768.0, None, A.mult, None, ["z2"], ["z"])
+            ts(T.iz0[:], T.iz[:], T.pcol[:, 1:2], None, A.mult, None, ["iz", "pc1"], ["iz0"])
+            ts(T.iz1[:], T.iz[:], T.pcol[:, 2:3], None, A.mult, None, ["iz", "pc2"], ["iz1"])
+            ts(T.sb[:], T.bd[:], T.pcol[:, 4:5], None, A.mult, None, ["bd", "pc4"], ["sb"])
+        feat_act(0)
+        feat_act(1)
+        feat_vec(0)
+        if t:
+            finish(t - 1, prev)
+        own_send(t, callee)
+        cand(t, 0, callee)
+        feat_vec(1)
+        cand(t, 1, callee)
+        expand(t, 0)
+        expand(t, 1)
+        own_side(t)
+        if t:
+            back(t - 1)
+        score(t)
+        partner(t)
+        meet(t, caller)
+        prev = caller
+    back(RO - 1)
+    dma("S", T.yent[:, 0:1024], T.raw[:, 0:1024], ["raw"], [], "dy")
+    dma("A", T.yent[:, 1024:2048], T.raw[:, 1024:2048], ["raw"], [], "dy")
+    for s in tot:
+        wait("G", [(s, tot[s], {})])
+
+
+SCRATCH["bcol"] = ("sbuf", [128, 4], "float32")

@@ -1,5 +1,4 @@
-from concourse.bass import DstId, RemoteDMATransfer
-from concourse.mybir import dt, AluOpType, AxisListType, ActivationFunctionType
+from concourse.mybir import AluOpType, ActivationFunctionType
 
 N = 8
 RO = 4
@@ -8,139 +7,36 @@ MB = M0 * 2048.0
 BIG = 1048576.0
 W = 2048 + 128
 NE = 8
+VS = 40
 
-SCRATCH = {
-    "ents": ("sbuf", [128, 2048], "int32"),
-    "raw": ("sbuf", [128, W], "float32"),
-    "cod": ("sbuf", [128, W], "float32"),
-    "st": ("sbuf", [128, 2048], "float32"),
-    "fw": ("sbuf", [128, 4112], "bfloat16"),
-    "cf1": ("sbuf", [128, 2048], "float32"),
-    "cf2": ("sbuf", [128, 2048], "float32"),
-    "wti": ("sbuf", [128, 4], "int32"),
-    "kpi": ("sbuf", [128, 4], "int32"),
-    "ones": ("sbuf", [128, 160], "bfloat16"),
-    "one16": ("sbuf", [128, 128], "bfloat16"),
-    "bd0": ("sbuf", [128, 128], "bfloat16"),
-    "bd": ("sbuf", [128, 128], "bfloat16"),
-    "z0": ("sbuf", [128, 144], "bfloat16"),
-    "z1": ("sbuf", [128, 144], "bfloat16"),
-    "z2": ("sbuf", [128, 144], "bfloat16"),
-    "z": ("sbuf", [128, 144], "bfloat16"),
-    "iz": ("sbuf", [128, 160], "bfloat16"),
-    "iz0": ("sbuf", [128, 160], "float16"),
-    "iz1": ("sbuf", [128, 160], "float16"),
-    "sb": ("sbuf", [128, 128], "float16"),
-    "wblk": ("sbuf", [128, 128], "bfloat16"),
-    "fm": ("sbuf", [128, 2048], "bfloat16"),
-    "cli": ("sbuf", [128, 128], "int32"),
-    "cl": ("sbuf", [128, 128], "uint16"),
-    "pi": ("sbuf", [128, 4], "int32"),
-    "pcol": ("sbuf", [128, 16], "float32"),
-    "p16": ("sbuf", [128, 4], "int32"),
-    "ii": ("sbuf", [128, 8], "int32"),
-    "ij": ("sbuf", [128, 8], "int32"),
-    "dum": ("sbuf", [128, 8], "float32"),
-    "dmc": ("sbuf", [128, 8], "float32"),
-    "dl3": ("sbuf", [128, 32], "float32"),
-    "ji": ("sbuf", [128, 16], "int32"),
-    "tri": ("sbuf", [128, 8, 16], "bfloat16"),
-    "sti": ("sbuf", [128, 64], "int32"),
-    "stj": ("sbuf", [128, 64], "int32"),
-    "i1": ("sbuf", [128, 128], "int32"),
-    "i2": ("sbuf", [128, 128], "int32"),
-    "i3": ("sbuf", [128, 128], "int32"),
-    "f4": ("sbuf", [128, 128], "float32"),
-    "f5": ("sbuf", [128, 128], "float32"),
-    "lst": ("sbuf", [128, 128], "uint16"),
-    "fg": ("sbuf", [128, 2048], "bfloat16"),
-    "fs": ("sbuf", [128, 2048], "bfloat16"),
-    "u1": ("sbuf", [128, 128], "int32"),
-    "u2": ("sbuf", [128, 128], "int32"),
-    "u3": ("sbuf", [128, 128], "float32"),
-    "u4": ("sbuf", [128, 128], "float32"),
-    "u5": ("sbuf", [128, 128], "int32"),
-    "u6": ("sbuf", [128, 128], "int32"),
-    "se": ("sbuf", [128, 512], "uint16"),
-    "le": ("sbuf", [128, 512], "uint16"),
-    "so": ("sbuf", [128, 1024], "float32"),
-    "lo": ("sbuf", [128, 1024], "float32"),
-    "sa": ("sbuf", [128, 16], "float32"),
-    "la": ("sbuf", [128, 16], "float32"),
-    "sx": ("sbuf", [128, 4 * 392], "float32"),
-    "ln": ("sbuf", [128, 4 * 264], "float32"),
-    "ox": ("sbuf", [128, 2048], "float32"),
-    "dd": ("sbuf", [128, 2048], "bfloat16"),
-    "da": ("sbuf", [128, 2048], "bfloat16"),
-    "db": ("sbuf", [128, 2048], "bfloat16"),
-    "mt": ("sbuf", [128, 2048], "bfloat16"),
-    "eb": ("sbuf", [128, 128], "float32"),
-    "key": ("sbuf", [128, 128], "float32"),
-    "kt": ("sbuf", [128, 128], "float32"),
-    "ks": ("sbuf", [128, 128], "float32"),
-    "kr": ("sbuf", [128, 128], "float32"),
-    "et": ("sbuf", [128, 128], "float16"),
-    "rt": ("sbuf", [128, 128], "float16"),
-    "row": ("sbuf", [128, 128], "float16"),
-    "eq": ("sbuf", [128, 8, 144], "bfloat16"),
-    "l1": ("sbuf", [128, 8], "uint16"),
-    "l2": ("sbuf", [128, 32], "uint16"),
-    "l3": ("sbuf", [128, 32], "uint16"),
-    "dl2": ("sbuf", [128, 8], "float32"),
-    "w2": ("sbuf", [128, 8], "float32"),
-    "w2b": ("sbuf", [128, 8], "float32"),
-    "w3": ("sbuf", [128, 8], "float32"),
-    "win": ("sbuf", [128, 128], "bfloat16"),
-    "wj": ("sbuf", [128, 128], "bfloat16"),
-    "cab": ("sbuf", [128, 4], "bfloat16"),
-    "ah": ("sbuf", [128, 128], "int32"),
-    "al": ("sbuf", [128, 128], "int32"),
-    "ak": ("sbuf", [128, 128], "int32"),
-    "an": ("sbuf", [128, 128], "float32"),
-    "av": ("sbuf", [128, 128], "float32"),
-    "aq": ("sbuf", [128, 128], "float32"),
-    "am": ("sbuf", [128, 128], "float32"),
-    "ti": ("sbuf", [128, 128], "float32"),
-    "ea": ("sbuf", [128, 128], "float32"),
-    "ef": ("sbuf", [128, 128], "float32"),
-    "c0": ("sbuf", [128, 128], "float32"),
-    "c1": ("sbuf", [128, 128], "float32"),
-    "bg": ("sbuf", [128, 128], "float32"),
-    "bh": ("sbuf", [128, 128], "int32"),
-    "bl": ("sbuf", [128, 128], "int32"),
-    "bk": ("sbuf", [128, 128], "int32"),
-    "bn": ("sbuf", [128, 128], "float32"),
-    "bv": ("sbuf", [128, 128], "float32"),
-    "bp": ("sbuf", [128, 128], "float32"),
-    "gb": ("sbuf", [128, 128], "float32"),
-    "di": ("sbuf", [128, 128], "float32"),
-    "dq": ("sbuf", [128, 128], "float32"),
-    "sm": ("sbuf", [128, 128], "float32"),
-    "t1": ("sbuf", [128, 128], "float32"),
-    "t1b": ("sbuf", [128, 128], "float32"),
-    "t1c": ("sbuf", [128, 128], "float32"),
-    "bq": ("sbuf", [128, 128], "float32"),
-    "bm": ("sbuf", [128, 128], "float32"),
-    "t2": ("sbuf", [128, 128], "float32"),
-    "t2b": ("sbuf", [128, 128], "float32"),
-    "mx": ("sbuf", [128, 128], "float32"),
-    "pp": ("sbuf", [128, 128], "float32"),
-    "x1": ("sbuf", [128, 256], "float32"),
-    "x2": ("sbuf", [128, 256], "float32"),
-    "ebz": ("sbuf", [128, 128], "float32"),
-    "nbc": ("sbuf", [128, 512], "float32"),
-    "psU": ("psum", [128, 512], "float32"),
-    "psK0": ("psum", [128, 512], "float32"),
-    "psK1": ("psum", [128, 512], "float32"),
-    "psL": ("psum", [128, 512], "float32"),
-    "psR": ("psum", [128, 512], "float32"),
-    "psC": ("psum", [128, 512], "float32"),
-    "psG": ("psum", [128, 512], "float32"),
-    "psV": ("psum", [128, 512], "float32"),
-}
+_F, _B, _I, _H, _U = "float32", "bfloat16", "int32", "float16", "uint16"
+SCRATCH = {}
+for _n, _w, _d in [
+        ("ents", 2048, _I), ("raw", W, _F), ("cod", W, _F), ("st", 2048, _F), ("fw", 4112, _B), ("cf1", 2048, _F), ("cf2", 2048, _F),
+        ("wti", 4, _I), ("kpi", 4, _I), ("bcol", 8, _F),
+        ("ones", 160, _B), ("one16", 128, _B), ("bd0", 128, _B), ("bd", 128, _B), ("z0", 144, _B), ("z1", 144, _B), ("z2", 144, _B),
+        ("z", 144, _B), ("zl", 144, _B), ("iz", 160, _B), ("iz0", 160, _H), ("iz1", 160, _H), ("sb", 128, _H), ("wblk", 128, _B),
+        ("fm", 2048, _B), ("cli", 128, _I), ("cl", 128, _U), ("pi", 4, _I), ("pcol", 16, _F), ("p16", 4, _I), ("ii", 8, _I),
+        ("dum", 8, _F), ("dmc", 8, _F), ("ji", 16, _I), ("sti", 64, _I), ("stj", 64, _I),
+        ("i1", 128, _I), ("i2", 128, _I), ("i3", 128, _I), ("lst", 128, _U), ("fg", 2048, _B), ("fs", 2048, _B),
+        ("u1", 128, _I), ("u2", 128, _I), ("u4", 128, _F), ("u5", 128, _I), ("u6", 128, _I),
+        ("se", 512, _U), ("le", 512, _U), ("so", 1024, _F), ("lo", 1024, _F), ("sa", 16, _F), ("la", 16, _F),
+        ("sx", 4 * 384, _F), ("ln", 4 * 256, _F), ("nbc", 512, _F), ("c1", 256, _F), ("c2", 256, _F), ("o1", 128, _F), ("o2", 128, _F),
+        ("ox", 2048, _F), ("dd", 2048, _B), ("da", 2048, _B), ("db", 2048, _B), ("mt", 2048, _B),
+        ("eb", 128, _F), ("key", 128, _F), ("kt", 128, _F), ("ks", 128, _F), ("et", 128, _H), ("rt", 128, _H),
+        ("l1", 8, _U), ("l2", 32, _U), ("dl2", 8, _F), ("w2", 8, _F), ("w2b", 8, _F),
+        ("win", 128, _B), ("wj", 128, _B), ("cab", 4, _B),
+        ("ah", 128, _I), ("al", 128, _I), ("ak", 128, _I), ("ap", 128, _F), ("as2", 128, _F), ("ad", 128, _F), ("ea", 128, _F),
+        ("ac1", 128, _F), ("ac2", 128, _F),
+        ("bg", 128, _F), ("bh", 128, _I), ("bl", 128, _I), ("bk", 128, _I), ("bs", 128, _F), ("bp", 128, _F), ("di", 128, _F),
+        ("dq", 128, _F), ("sg", 128, _F), ("ebz", 128, _F), ("bd2", 128, _F), ("t2b", 128, _F), ("pp", 128, _F), ("d2", 128, _F)]:
+    SCRATCH[_n] = ("sbuf", [128, _w], _d)
+SCRATCH["tri"] = ("sbuf", [128, 8, 16], _B)
+SCRATCH["eq"] = ("sbuf", [128, 8, 144], _B)
+for _n in ("psU", "psK0", "psK1", "psL", "psR", "psC", "psG", "psV"):
+    SCRATCH[_n] = ("psum", [128, 512], _F)
 SEMAPHORES = (["sV", "sA", "sP", "sG", "dent", "dsm", "dfe", "dst", "dy", "loc"]
-              + ["ro%d" % t for t in range(RO)] + ["re%d%d" % (t, h) for t in range(RO) for h in range(2)]
-              + ["rn%d" % t for t in range(RO)] + ["ra%d" % t for t in range(RO)])
+              + ["%s%d" % (k, t) for k in ("ro", "re", "rn", "ra") for t in range(RO)])
 
 
 def rank_program(g, core, T, topo):
@@ -152,15 +48,15 @@ def rank_program(g, core, T, topo):
     Q = {"V": g.vector, "A": g.scalar, "P": g.tensor, "G": g, "S": g.sync}
     tot = {}
     seen = {"V": {}, "A": {}, "P": {}, "G": {}, "S": {}}
-    wr, rd = {}, {}
+    wr, rd, bank = {}, {}, {}
     v, a, pe = g.vector, g.scalar, g.tensor
 
     def wait(q, evs):
         evs = [e for e in evs if seen[q].get(e[0], 0) < e[1]]
-        for i, e in enumerate(evs):
+        for e in evs:
             if seen[q].get(e[0], 0) >= e[1]:
                 continue
-            if any(o is not e and o[2].get(e[0], 0) >= e[1] for o in evs):
+            if any(o is not e and o[2].get(e[0], 0) >= e[1] and (o[0] != e[0] or o[1] > e[1]) for o in evs):
                 continue
             Q[q].wait_ge(T.sem[e[0]], e[1])
             seen[q][e[0]] = e[1]
@@ -169,29 +65,30 @@ def rank_program(g, core, T, topo):
                 if seen[q].get(s, 0) < n:
                     seen[q][s] = n
 
-    def deps(q, r, w, dma):
+    def deps(q, r, w):
         evs = []
         for k in r:
             evs += [e for o, e in wr.get(k, [])]
-            if k[:2] == "ps":
-                evs += [e for o, e in rd.get(k, []) if o != q]
         for k in w:
-            evs += [e for o, e in wr.get(k, []) if not (q == "P" and o == "P")]
-            evs += [e for o, e in rd.get(k, []) if dma or o != q]
+            evs += [e for o, e in wr.get(k, []) if o != q]
+            evs += [e for o, e in rd.get(k, []) if o != q]
+        for k in list(r) + list(w):
+            if k[:2] == "ps":
+                evs += [e for o, e in bank.get(k.split(":")[0], {}).items() if o != q]
         return evs
 
     def note(q, r, w, ev):
         for k in w:
-            if q == "P" and wr.get(k) and wr[k][0][0] == "P":
-                wr[k] = [(q, ev)]
-            else:
-                wr[k] = [(q, ev)]
+            wr[k] = [(q, ev)]
             rd[k] = []
         for k in r:
             rd[k] = [x for x in rd.get(k, []) if x[0] != q or q == "D"] + [(q, ev)]
+        for k in list(r) + list(w):
+            if k[:2] == "ps":
+                bank.setdefault(k.split(":")[0], {})[q] = ev
 
-    def op(q, fn, r, w, x=()):
-        wait(q, deps(q, r, w, False) + list(x))
+    def op(q, fn, r, w):
+        wait(q, deps(q, r, w))
         s = "s" + q
         tot[s] = tot.get(s, 0) + 1
         fn().then_inc(T.sem[s], 1)
@@ -200,7 +97,7 @@ def rank_program(g, core, T, topo):
         note(q, r, w, (s, tot[s], clk))
 
     def dma(q, out, in_, r, w, s):
-        wait(q, deps(q, r, w, True))
+        wait(q, deps("D" + q, r, w))
         Q[q].dma_start(out, in_).then_inc(T.sem[s], 16)
         tot[s] = tot.get(s, 0) + 16
         clk = dict(seen[q])
@@ -211,7 +108,7 @@ def rank_program(g, core, T, topo):
         wr[k] = [("D", (s, tot[s], {s: tot[s]}))]
 
     def send(dst, out, in_, r, s):
-        wait("G", deps("G", r, [], True))
+        wait("G", deps("G", r, []))
         rid, pid = topo.addr(dst)[:2]
         m = 0
         for e in topo.engines(core, dst)[:NE]:
@@ -244,154 +141,170 @@ def rank_program(g, core, T, topo):
     def ms(ap, c, w):
         op("V", lambda: v.memset(ap, c), [], w)
 
-    dma("S", T.ents[:, 0:1024], T.ent[:, 0:1024], [], ["ents"], "dent")
+    BC = {}
+
+    def bias(c):
+        if c not in BC:
+            i = len(BC)
+            BC[c] = i
+            ms(T.bcol[:, i:i + 1], c, ["bc%d" % i])
+        return T.bcol[:, BC[c]:BC[c] + 1]
+
+    dma("S", T.ents[:, 0:1024], T.ent[:, 0:1024], [], [], "dent")
     dma("A", T.ents[:, 1024:2048], T.ent[:, 1024:2048], [], [], "dent")
     joined("ents", "dent")
+    dma("S", T.wti[:, 0:1], T.wt[:, 0:1], [], [], "dsm")
+    dma("A", T.kpi[:, 0:1], T.kap[:, 0:1], [], [], "dsm")
+    joined("wti", "dsm")
+    joined("kpi", "dsm")
     dma("S", T.fw[:, 0:2048], T.feat[:, 0:2048], [], [], "dfe")
     dma("A", T.fw[:, 2048:4096], T.feat[:, 2048:4096], [], [], "dfe")
     joined("fw", "dfe")
-    dma("S", T.wti[:, 0:1], T.wt[:, 0:1], [], [], "dsm")
-    dma("S", T.kpi[:, 0:1], T.kap[:, 0:1], [], [], "dsm")
-    joined("wti", "dsm")
-    joined("kpi", "dsm")
 
     ms(T.ones[:], 1.0, ["ones"])
-    op("G", lambda: g.iota(T.pi[:, 0:1], [[1, 1]], 0, 1), [], ["pi"])
-    op("G", lambda: g.iota(T.cli[:], [[1, 128]], 0, 0), [], ["cli"])
     op("G", lambda: g.iota(T.sti[:], [[37, 64]], 0, 0), [], ["sti"])
+    op("G", lambda: g.iota(T.pi[:, 0:1], [[1, 1]], 0, 1), [], ["pi"])
     op("G", lambda: g.affine_select(T.bd0[:], T.ones[:, 0:128], [[-16, 8], [0, 16]], A.is_ge, 0.0, 0, 1), ["ones"], ["bd0"])
     op("G", lambda: g.affine_select(T.bd[:], T.bd0[:], [[16, 8], [0, 16]], A.is_ge, 0.0, 15, -1), ["bd0"], ["bd"])
-    op("G", lambda: g.iota(T.ii[:], [[16, 8]], 2048, 0), [], ["ii"])
-    op("G", lambda: g.iota(T.ij[:], [[256, 8]], 0, 0), [], ["ij"])
-    op("G", lambda: g.iota(T.ji[:], [[1, 16]], 0, 0), [], ["ji"])
+    op("G", lambda: g.iota(T.cli[:], [[1, 128]], 0, 0), [], ["cli"])
     op("G", lambda: g.affine_select(T.z0[:], T.ones[:, 0:144], [[-16, 9], [0, 16]], A.is_ge, 0.0, 0, 1), ["ones"], ["z0"])
     op("G", lambda: g.affine_select(T.z1[:], T.z0[:], [[16, 9], [0, 16]], A.is_ge, 0.0, 15, -1), ["z0"], ["z1"])
     op("G", lambda: g.affine_select(T.z2[:], T.z1[:], [[0, 9], [1, 16]], A.is_equal, 0.0, -15, 0), ["z1"], ["z2"])
     op("G", lambda: g.affine_select(T.iz[:], T.ones[:], [[-1, 160]], A.is_equal, 0.0, 16, 1), ["ones"], ["iz"])
-    ms(T.fw[:, 4096:4112], 0.0, ["fwz"])
+    op("G", lambda: g.iota(T.ii[:], [[16, 8]], 2048, 0), [], ["ii"])
+    op("G", lambda: g.iota(T.ji[:], [[1, 16]], 0, 0), [], ["ji"])
+    b_w, b_f, b_w1, b_mb, b_g, b_64, b_ea = [bias(c) for c in (-8.5, M0, -1024.5, MB, -MB / 16, -64.0, 1.0 / BIG)]
+    b_one = bias(1.0)
+    wait("A", [wr["bc%d" % i][0][1] for i in range(len(BC))])
     ms(T.fm[:], 1.0, ["fm"])
-    ms(T.fm[:, 0:2048:16], 0.0, ["fm"])
-    ms(T.one16[:], 0.0625, ["one16"])
+    op("V", lambda: v.memset(T.fm[:, 0:2048:16], 0.0), ["fm"], ["fm"])
+    ms(T.fw[:, 4096:4112], 0.0, ["fwz"])
     ms(T.pcol[:, 8:9], -0.375, ["acol"])
-    ms(T.sa[:], 0.0, ["sa"])
+    ts(T.stj[:], T.sti[:], 63, None, A.bitwise_and, None, ["sti"], ["stj"])
     ts(T.p16[:, 0:1], T.pi[:, 0:1], 15, None, A.bitwise_and, None, ["pi"], ["p16"])
     ts(T.p16[:, 1:2], T.pi[:, 0:1], 16, None, A.bitwise_and, None, ["pi"], ["p16b"])
-    vc(T.pcol[:, 0:1], T.p16[:, 0:1], ["p16"], ["pc0"])
-    ts(T.pcol[:, 1:2], T.p16[:, 1:2], 0.0, None, A.is_equal, None, ["p16b"], ["pc1"])
-    ts(T.pcol[:, 2:3], T.p16[:, 1:2], 0.0, None, A.is_gt, None, ["p16b"], ["pc2"])
-    ts(T.pcol[:, 3:4], T.p16[:, 0:1], -2048.0, 15 * 2048 - 1023.5, A.mult, A.add, ["p16"], ["pc3"])
-    ts(T.pcol[:, 4:5], T.p16[:, 0:1], 15.0, None, A.is_equal, None, ["p16"], ["pc4"])
-    ts(T.pcol[:, 5:6], T.p16[:, 0:1], 16.0, None, A.mult, None, ["p16"], ["pc5"])
-    vc(T.cl[:], T.cli[:], ["cli"], ["cl"])
-    ts(T.stj[:], T.sti[:], 63, None, A.bitwise_and, None, ["sti"], ["stj"])
     ts(T.st[:, 0:64], T.stj[:], 2048.0, -17.0, A.mult, A.add, ["stj"], ["st"])
-    ts(T.dum[:], T.ii[:], T.pcol[:, 0:1], None, A.add, None, ["ii", "pc0"], ["dum"])
-    ts(T.dmc[:], T.dum[:], -1023.5, None, A.add, None, ["dum"], ["dmc"])
-    ts(T.w3[:], T.ij[:], T.pcol[:, 5:6], None, A.add, None, ["ij", "pc5"], ["w3"])
-    tt(T.w2[:], T.w3[:], T.dum[:], A.subtract, ["w3", "dum"], ["w2"])
-    for t in range(RO):
-        ts(T.dl3[:, 8 * t:8 * t + 8], T.w2[:], float(t), None, A.add, None, ["w2"], ["dl3"])
-    for c in range(8):
-        ts(T.tri[:, c, 0:16], T.ji[:], T.pcol[:, 0:1], None, A.is_gt, None, ["ji", "pc0"], ["tri"])
+    ts(T.pcol[:, 3:4], T.p16[:, 0:1], -2048.0, 15 * 2048 - 1023.5, A.mult, A.add, ["p16"], ["pc3"])
+    vc(T.cl[:], T.cli[:], ["cli"], ["cl"])
+    vc(T.pcol[:, 6:7], T.wti[:, 0:1], ["wti"], ["wcol"])
+    vc(T.pcol[:, 7:8], T.kpi[:, 0:1], ["kpi"], ["kcol"])
+    ts(T.wblk[:], T.bd[:], T.pcol[:, 6:7], None, A.mult, None, ["bd", "wcol"], ["wblk"])
     n = 64
     while n < 2048:
         dma("S", T.st[:, n:2 * n], T.st[:, 0:n], ["st"], ["st"], "dst")
         n *= 2
 
-    def first_table():
-        banks = ["psK0", "psK1", "psR", "psC"]
+    def more_constants():
+        ms(T.one16[:], 0.0625, ["one16"])
+        ms(T.sa[:], 0.0, ["sa"])
+        vc(T.pcol[:, 0:1], T.p16[:, 0:1], ["p16"], ["pc0"])
+        ts(T.pcol[:, 1:2], T.p16[:, 1:2], 0.0, None, A.is_equal, None, ["p16b"], ["pc1"])
+        ts(T.pcol[:, 2:3], T.p16[:, 1:2], 0.0, None, A.is_gt, None, ["p16b"], ["pc2"])
+        ts(T.pcol[:, 4:5], T.p16[:, 0:1], 15.0, None, A.is_equal, None, ["p16"], ["pc4"])
+        ts(T.zl[:], T.z2[:], 0.0625, None, A.mult, None, ["z2"], ["zl"])
+        ts(T.iz0[:], T.iz[:], T.pcol[:, 1:2], None, A.mult, None, ["iz", "pc1"], ["iz0"])
+        ts(T.iz1[:], T.iz[:], T.pcol[:, 2:3], None, A.mult, None, ["iz", "pc2"], ["iz1"])
+        ts(T.sb[:], T.bd[:], T.pcol[:, 4:5], None, A.mult, None, ["bd", "pc4"], ["sb"])
+        ts(T.dum[:], T.ii[:], T.pcol[:, 0:1], None, A.add, None, ["ii", "pc0"], ["dum"])
+        yield
+        for c in range(8):
+            ts(T.tri[:, c, 0:16], T.ji[:], T.pcol[:, 0:1], None, A.is_gt, None, ["ji", "pc0"], ["tri"])
+        yield
+        ts(T.dmc[:], T.dum[:], -1023.5, None, A.add, None, ["dum"], ["dmc"])
+
+    banks = ["psK0", "psK1", "psR", "psC"]
+
+    def first_raw():
         for i in range(4):
             s = slice(512 * i, 512 * i + 512)
             k = "@%d" % i
             vc(T.raw[:, s], T.ents[:, s], ["ents"], ["raw" + k])
+            act(T.cf2[:, s], T.raw[:, s], F.Identity, ["raw" + k], ["cf2" + k], bias=b_w)
+            act(T.cf2[:, s], T.cf2[:, s], F.Identity, ["cf2" + k], ["cf2" + k], bias=b_f, scale=0.0625)
             ts(T.cf1[:, s], T.ents[:, s], -1024.5, MB, A.add, A.add, ["ents"], ["cf1" + k])
-            act(T.cf2[:, s], T.raw[:, s], F.Identity, ["raw" + k], ["cf2" + k], bias=T.bcol[:, 0:1])
-            act(T[banks[i]][:], T.cf1[:, s], F.Identity, ["cf1" + k], [banks[i]], bias=T.bcol[:, 1:2], scale=0.0625)
-            act(T.cf2[:, s], T.cf2[:, s], F.Identity, ["cf2" + k], ["cf2" + k], bias=T.bcol[:, 2:3], scale=0.0625)
-        for i in range(4):
-            s = slice(512 * i, 512 * i + 512)
-            k = "@%d" % i
-            tt(T.cod[:, s], T[banks[i]][:], T.cf2[:, s], A.add, [banks[i], "cf2" + k], ["code"] if i == 3 else [])
-            wr["code"] = wr.get("code", [])
+            act(T[banks[i]][:], T.cf1[:, s], F.Identity, ["cf1" + k], [banks[i]], bias=b_g, scale=0.0625)
         wr["raw"] = list(wr["raw@3"])
 
-    ms(T.bcol[:, 0:1], -8.5, ["bc0"])
-    ms(T.bcol[:, 1:2], -MB / 16, ["bc1"])
-    ms(T.bcol[:, 2:3], M0, ["bc2"])
-    ms(T.bcol[:, 3:4], -64.0, ["bc3"])
-    wait("A", [wr[k][0][1] for k in ("bc0", "bc1", "bc2", "bc3")])
+    def first_cod():
+        for i in range(4):
+            s = slice(512 * i, 512 * i + 512)
+            tt(T.cod[:, s], T[banks[i]][:], T.cf2[:, s], A.add, [banks[i], "cf2@%d" % i], ["cod"])
 
-    VS = 24
-    WC = 4112
-    keys = {"lists": ["fw", "fwz"]}
+    def code_parts(src, sk, t1, t2, k, ps):
+        act(t2, src, F.Identity, sk, [k + "2"], bias=b_w)
+        act(t1, src, F.Identity, sk, [k + "1"], bias=b_w1)
+        act(t2, t2, F.Identity, [k + "2"], [k + "2"], bias=b_f, scale=0.0625)
+        act(t1, t1, F.Identity, [k + "1"], [k + "1"], bias=b_mb)
+        act(ps, t1, F.Identity, [k + "1"], [("psG:" if k == "n" else "psL:") + k], bias=b_g, scale=0.0625)
 
     def lane_list(t):
         src, sk = (T.ents, "ents") if t == 0 else (T.raw, "raw")
         ts(T.i1[:], src[:, t:2048:16], -1.0, None, A.add, None, [sk], ["i1"])
-        ts(T.i2[:], T.i1[:], 11, None, A.arith_shift_right, None, ["i1"], ["i2"])
         ts(T.i3[:], T.i1[:], 16, None, A.bitwise_and, None, ["i1"], ["i3"])
-        ts(T.f4[:], T.i3[:], 512.0, None, A.mult, None, ["i3"], ["f4"])
-        tt(T.f5[:], T.i2[:], T.f4[:], A.add, ["i2", "f4"], ["f5"])
-        ts(T.lst[:], T.f5[:], 4096.0, None, A.min, None, ["f5"], ["lst"])
+        ts(T.i2[:], T.i1[:], 11, None, A.arith_shift_right, None, ["i1"], ["i2"])
+        ts(T.psV[:, 0:128], T.i3[:], 512.0, None, A.mult, None, ["i3"], ["psV:1"])
+        tt(T.psV[:, 128:256], T.i2[:], T.psV[:, 0:128], A.add, ["i2", "psV:1"], ["psV:2"])
+        ts(T.lst[:], T.psV[:, 128:256], 4096.0, None, A.min, None, ["psV:2"], ["lst"])
 
-    def feat_act(h):
-        l0, l1 = 64 * h + VS, 64 * h + 64
-        op("A", lambda: a.activation(T.fg[:, 16 * l0:16 * l1], T.fw[:, 0:WC].indirect(T.lst[:, l0:l1]), F.Copy),
-           ["lst"] + keys["lists"], ["fgA%d" % h])
-
-    def feat_vec(h):
-        l0, l1 = 64 * h, 64 * h + VS
-        op("V", lambda: v.tensor_copy(T.fg[:, 16 * l0:16 * l1], T.fw[:, 0:WC].indirect(T.lst[:, l0:l1])),
-           ["lst"] + keys["lists"], ["fgV%d" % h])
-        for n0, n1, k in ((l0, l1, "V"), (l1, 64 * h + 64, "A")):
-            c = slice(16 * n0, 16 * n1)
-            op("V", lambda: v.tensor_tensor_scan(T.fs[:, c], T.fm[:, c], T.fg[:, c], 0.0, A.mult, A.max),
-               ["fm", "fg%s%d" % (k, h)], ["fs%d" % h])
-        mm(T.psU[:, 64 * h:64 * h + 64], T.wblk[:], T.fs[:, 1024 * h + 15:1024 * h + 1024:16], True, True,
-           ["wblk", "fs%d" % h], ["psU"])
-
-    def cand(t, h, dst):
-        s = slice(64 * h, 64 * h + 64)
-        o = 128 * t + 64 * h
-        ac = T.pcol[:, 8:9] if t == 0 else T.la[:, 4 * t - 4:4 * t - 3]
-        vc(T.u1[:, s], T.psU[:, s], ["psU"], ["u1"])
-        ts(T.u2[:, s], T.u1[:, s], 4095, None, A.bitwise_and, None, ["u1"], ["u2"])
-        ts(T.u3[:, s], T.u2[:, s], 0.03125, T.pcol[:, 7:8], A.mult, A.add, ["u2", "kcol"], ["u3"])
-        tt(T.u4[:, s], T.u3[:, s], T.u2[:, s], A.mult, ["u3", "u2"], ["u4"])
-        ts(T.u5[:, s], T.u4[:, s], ac, None, A.add, None, ["u4", "acol" if t == 0 else "la%d" % (t - 1)], ["u5"])
-        ts(T.u6[:, s], T.u5[:, s], 2047, None, A.bitwise_and, None, ["u5"], ["u6"])
-        vc(T.se[:, o:o + 64], T.u6[:, s], ["u6"], ["se%d%d" % (t, h)])
-        send(dst, T.le[:, o:o + 64], T.se[:, o:o + 64], ["se%d%d" % (t, h)], "re%d%d" % (t, h))
+    def own_parts(t):
+        o = 256 * t
+        if t == 0:
+            vc(T.so[:, 0:128], T.ents[:, 0:2048:16], ["ents"], ["so0"])
+        else:
+            act(T.so[:, o:o + 128], T.raw[:, t:2048:16], F.Copy, ["raw"], ["so%d" % t])
+        code_parts(T.so[:, o:o + 128], ["so%d" % t], T.o1[:], T.o2[:], "o", T.psL[:, 256:384])
 
     def own_send(t, dst):
         o = 256 * t
-        act(T.so[:, o:o + 128], T.raw[:, t:2048:16], F.Copy, ["raw"], ["so%da" % t])
-        act(T.so[:, o + 128:o + 256], T.cod[:, t:2048:16], F.Copy, ["code"], ["so%db" % t])
-        send(dst, T.lo[:, o:o + 256], T.so[:, o:o + 256], ["so%da" % t, "so%db" % t], "ro%d" % t)
+        tt(T.so[:, o + 128:o + 256], T.psL[:, 256:384], T.o2[:], A.add, ["psL:o", "o2"], ["soc%d" % t])
+        send(dst, T.lo[:, o:o + 256], T.so[:, o:o + 256], ["so%d" % t, "soc%d" % t], "ro%d" % t)
 
-    def scatter(tab, lists, vals, r, w):
-        op("V", lambda: v.tensor_copy(T[tab][:, 0:W].indirect(lists), vals), r, w)
+    def features():
+        rk = ["lst", "fw", "fwz"]
+        op("A", lambda: a.activation(T.fg[:, 16 * VS:2048], T.fw[:].indirect(T.lst[:, VS:128]), F.Copy), rk, ["fgA"])
+        op("V", lambda: v.tensor_copy(T.fg[:, 0:16 * VS], T.fw[:].indirect(T.lst[:, 0:VS])), rk, ["fgV"])
+
+    def scans(t):
+        for n0, n1, k in ((0, VS, "V"), (VS, 128, "A")):
+            c = slice(16 * n0, 16 * n1)
+            op("V", lambda: v.tensor_tensor_scan(T.fs[:, c], T.fm[:, c], T.fg[:, c], 0.0, A.mult, A.max), ["fm", "fg" + k], ["fs" + k])
+        mm(T.psU[:, 0:128], T.wblk[:], T.fs[:, 15:2048:16], True, True, ["wblk", "fsV", "fsA"], ["psU"])
+
+    def cand(t, dst):
+        o = 128 * t
+        ac, ak = (T.pcol[:, 8:9], "acol") if t == 0 else (T.la[:, 4 * t - 4:4 * t - 3], "la%d" % (t - 1))
+        vc(T.u1[:], T.psU[:, 0:128], ["psU"], ["u1"])
+        ts(T.u2[:], T.u1[:], 4095, None, A.bitwise_and, None, ["u1"], ["u2"])
+        ts(T.psV[:, 0:128], T.u2[:], 0.03125, T.pcol[:, 7:8], A.mult, A.add, ["u2", "kcol"], ["psV:1"])
+        tt(T.u4[:], T.psV[:, 0:128], T.u2[:], A.mult, ["psV:1", "u2"], ["u4"])
+        ts(T.u5[:], T.u4[:], ac, None, A.add, None, ["u4", ak], ["u5"])
+        ts(T.u6[:], T.u5[:], 2047, None, A.bitwise_and, None, ["u5"], ["u6"])
+        vc(T.se[:, o:o + 128], T.u6[:], ["u6"], ["se%d" % t])
+        send(dst, T.le[:, o:o + 128], T.se[:, o:o + 128], ["se%d" % t], "re%d" % t)
+
+    def scatter(tab, lists, vals, r):
+        op("V", lambda: v.tensor_copy(T[tab][:].indirect(lists), vals), r, [tab])
 
     def own_side(t):
         o = 256 * t
-        th, ck = 8.0 + t, 12.0 + t
+        th = 8.0 + t
         av, lk = T.lo[:, o:o + 128], "lo%d" % t
         tt(T.ah[:], av, T.st[:, t:2048:16], A.add, [lk, "st"], ["ah"])
         ts(T.al[:], T.ah[:], 31, None, A.bitwise_and, None, ["ah"], ["al"])
         ts(T.ak[:], T.ah[:], 114688, None, A.bitwise_and, None, ["ah"], ["ak"])
-        ts(T.an[:], T.al[:], th, BIG, A.is_ge, A.mult, ["al"], ["an"])
-        tt(T.av[:], T.ak[:], T.an[:], A.is_le, ["ak", "an"], ["av"])
-        tt(T.psV[:, 0:128], av, T.av[:], A.mult, [lk, "av"], ["psV"])
-        ts(T.aq[:], T.al[:], -1.0, ck, A.mult, A.add, ["al"], ["aq"])
-        ts(T.am[:], T.al[:], th, None, A.is_lt, None, ["al"], ["am"])
-        ts(T.ea[:], T.psV[:, 0:128], 0.0, 1.0 / BIG, A.is_equal, A.mult, ["psV"], ["ea"])
-        ts(T.ef[:], T.psV[:, 0:128], 0.0, -16.0 * BIG, A.is_equal, A.mult, ["psV"], ["ef"])
-        ts(T.c0[:], av, -1024.5, MB, A.add, A.add, [lk], ["c0"])
-        ts(T.c1[:], T.c0[:], -MB, 1024.5, A.add, A.add, ["c0"], ["c1"])
-        ts(T.ti[:], T.al[:], 16.0, th, A.is_ge, A.mult, ["al"], ["ti"])
-        tt(T.psV[:, 128:256], T.aq[:], T.am[:], A.mult, ["aq", "am"], ["psV"])
-        tt(T.psV[:, 256:384], T.c1[:], T.ef[:], A.add, ["c1", "ef"], ["psV"])
-        tt(T.psV[:, 384:512], av, T.an[:], A.mult, [lk, "an"], ["psV"])
+        ts(T.psV[:, 0:128], T.al[:], th, BIG, A.is_ge, A.mult, ["al"], ["psV:1"])
+        ts(T.psV[:, 256:384], T.al[:], 16.0, None, A.is_ge, None, ["al"], ["psV:ia"])
+        tt(T.psV[:, 128:256], T.ak[:], T.psV[:, 0:128], A.is_le, ["ak", "psV:1"], ["psV:2"])
+        tt(T.as2[:], T.al[:], T.psV[:, 0:128], A.add, ["al", "psV:1"], ["as2"])
+        tt(T.psV[:, 384:512], av, T.psV[:, 0:128], A.mult, [lk, "psV:1"], ["psV:ga"])
+        tt(T.ap[:], av, T.psV[:, 128:256], A.mult, [lk, "psV:2"], ["ap"])
+
+    def own_side_scalar(t):
+        act(T.ad[:], T.as2[:], F.Relu, ["as2"], ["ad"], bias=b_ck[t], scale=-1.0)
+        act(T.ac1[:], T.ap[:], F.Identity, ["ap"], ["ac1"], bias=b_w1)
+        act(T.ea[:], T.ap[:], F.Relu, ["ap"], ["ea"], bias=b_ea, scale=-1.0 / BIG)
+        act(T.ac2[:], T.ac1[:], F.Identity, ["ac1"], ["ac2"], bias=b_mb)
+        act(T.psG[:, 384:512], T.ac2[:], F.Identity, ["ac2"], ["psG:c"], bias=b_mmb)
 
     def expand(t, h):
         o = 256 * t + 128
@@ -399,49 +312,58 @@ def rank_program(g, core, T, topo):
                                      T.lo[:, o:o + 128].indirect(T.cl[:, 64 * h:64 * h + 64]), F.Copy),
            ["lo%d" % t, "cl"], ["ox%d" % h])
 
+    CH = [0, 32, 64, 104, 128]
+    todo = [more_constants()]
+
+    def fill():
+        if todo:
+            next(todo[0], None)
+
     def score(t):
         def gat(i):
-            c = slice(512 * i, 512 * i + 512)
-            o = 128 * t + 32 * i
-            op("V", lambda: v.tensor_tensor(T.dd[:, c], T.cod[:, 0:2048].indirect(T.le[:, o:o + 32]), T.ox[:, c], A.subtract),
-               ["code", "le%d%d" % (t, i // 2), "ox%d" % (i // 2)], ["dd%d" % i])
+            c = slice(16 * CH[i], 16 * CH[i + 1])
+            o = 128 * t
+            op("V", lambda: v.tensor_tensor(T.dd[:, c], T.cod[:, 0:2048].indirect(T.le[:, o + CH[i]:o + CH[i + 1]]), T.ox[:, c], A.subtract),
+               ["cod", "le%d" % t, "ox%d" % (i // 2)], ["dd%d" % i])
             act(T.da[:, c], T.dd[:, c], F.Abs, ["dd%d" % i], ["da%d" % i])
-            act(T.db[:, c], T.da[:, c], F.Abs, ["da%d" % i], ["db%d" % i], bias=T.bcol[:, 3:4])
+            act(T.db[:, c], T.da[:, c], F.Abs, ["da%d" % i], ["db%d" % i], bias=b_64)
 
         def thr(i):
-            c = slice(512 * i, 512 * i + 512)
+            c = slice(16 * CH[i], 16 * CH[i + 1])
             ts(T.mt[:, c], T.db[:, c], 63.75, None, A.is_lt, None, ["db%d" % i], ["mt%d" % i])
 
         def add(h):
             k = "psK%d" % h
             for m in range(16):
                 mm(T[k][:, 0:64], T.z[:, 15 - m:143 - m], T.mt[:, 1024 * h + m:1024 * h + 1024:16], m == 0, m == 15,
-                   ["z", "mt%d" % (2 * h), "mt%d" % (2 * h + 1)], [k])
+                   ["z", "mt%d" % (2 * h), "mt%d" % (2 * h + 1)], [k + ":k"])
 
         def keyh(h):
             s = slice(64 * h, 64 * h + 64)
-            tt(T.key[:, s], T["psK%d" % h][:, 0:64], T.eb[:, s], A.add, ["psK%d" % h, "eb%d" % h], ["key%d" % h])
+            tt(T.key[:, s], T["psK%d" % h][:, 0:64], T.eb[:, s], A.add, ["psK%d:k" % h, "eb"], ["key%d" % h])
 
-        for h in range(2):
-            s = slice(64 * h, 64 * h + 64)
-            o = 128 * t + 64 * h
-            ts(T.eb[:, s], T.le[:, o:o + 64], T.pcol[:, 3:4], None, A.add, None, ["le%d%d" % (t, h), "pc3"], ["eb%d" % h])
-            gat(2 * h)
-            if h:
-                thr(1)
-                add(0)
-            gat(2 * h + 1)
-            thr(2 * h)
+        gat(0)
+        gat(1)
+        ts(T.eb[:], T.le[:, 128 * t:128 * t + 128], T.pcol[:, 3:4], None, A.add, None, ["le%d" % t, "pc3"], ["eb"])
+        fill()
+        thr(0)
+        gat(2)
+        thr(1)
+        add(0)
+        gat(3)
+        thr(2)
         keyh(0)
+        fill()
         thr(3)
         add(1)
+        fill()
         keyh(1)
 
     def partner(t):
         op("V", lambda: v.transpose(T.kt[:], T.key[:]), ["key0", "key1"], ["kt"])
         op("V", lambda: v.tensor_tensor_scan(T.ks[:], T.fm[:, 0:128], T.kt[:], 0.0, A.mult, A.max), ["fm", "kt"], ["ks"])
-        ts(T.kr[:], T.ks[:], MB, -MB, A.add, A.add, ["ks"], ["kr"])
-        tt(T.et[:], T.ks[:], T.kr[:], A.subtract, ["ks", "kr"], ["et"])
+        ts(T.psK1[:, 0:128], T.ks[:], MB, -MB, A.add, A.add, ["ks"], ["psK1:0"])
+        tt(T.et[:], T.ks[:], T.psK1[:, 0:128], A.subtract, ["ks", "psK1:0"], ["et"])
         for h in range(2):
             for g2 in range(2):
                 b = 16 - 16 * (g2 - h)
@@ -450,137 +372,148 @@ def rank_program(g, core, T, topo):
         op("V", lambda: v.transpose(T.rt[:], T.et[:]), ["et"], ["rt"])
         mm(T.psR[:, 0:128], T.sb[:], T.rt[:], True, True, ["sb", "rt"], ["psR"])
         ts(T.l1[:], T.psL[:, 0:8], 1023.5, None, A.add, None, ["psL"], ["l1"])
-        vc(T.row[:], T.psR[:, 0:128], ["psR"], ["row"])
+        tt(T.dl2[:], T.psL[:, 0:8], T.dmc[:], A.subtract, ["psL", "dmc"], ["dl2"])
         for c in range(8):
-            op("V", lambda: v.tensor_scalar(T.eq[:, c, 0:128 - 16 * c], T.row[:, 16 * c:128], T.psL[:, c:c + 1], None, A.is_equal),
-               ["row", "psL"], ["eq"])
+            op("V", lambda: v.tensor_scalar(T.eq[:, c, 0:128 - 16 * c], T.psR[:, 16 * c:128], T.psL[:, c:c + 1], None, A.is_equal),
+               ["psR", "psL"], ["eq"])
+        op("V", lambda: v.tensor_copy(T.bg[:], T.raw[:, 0:2048].indirect(T.l1[:])), ["raw", "l1"], ["bg"])
         tt(T.eq[:, :, 0:16], T.eq[:, :, 0:16], T.tri[:], A.mult, ["eq", "tri"], ["eq"])
         for c in range(8):
             mm(T.psC[:, 16 * c:128], T.bd[:], T.eq[:, c, 0:128 - 16 * c], c == 0, c == 7, ["bd", "eq"], ["psC"])
-        op("V", lambda: v.tensor_copy(T.bg[:], T.raw[:, 0:2048].indirect(T.l1[:])), ["raw", "l1"], ["bg"])
-        op("V", lambda: v.tensor_tensor(T.bh[:], T.st[:, 0:2048].indirect(T.l1[:]), T.bg[:], A.add), ["st", "l1", "bg"], ["bh"])
-        tt(T.dl2[:], T.psL[:, 0:8], T.dmc[:], A.subtract, ["psL", "dmc"], ["dl2"])
-        ts(T.win[:], T.psC[:, 0:128], 0.5, 2.0 ** -19, A.is_lt, A.mult, ["psC"], ["win"])
-        for s in range(16):
-            mm(T.psC[:, 128:136], T.z[:, 15 - s:143 - s], T.win[:, s:128:16], s == 0, s == 15, ["z", "win"], ["psC"])
-        if t < RO - 1:
-            op("A", lambda: a.activation(T.wj[:], T.win[:], F.Copy, scale=2.0 ** 19, accum_out=T.pcol[:, 9:10]), ["win"], ["wj", "ca"])
-            act(T.cab[:, 0:1], T.pcol[:, 9:10], F.Copy, ["ca"], ["cab"])
-            mm(T.psC[:, 136:137], T.one16[:], T.cab[:, 0:1], True, True, ["one16", "cab"], ["psC"])
+        op("V", lambda: v.tensor_tensor(T.bh[:], T.st[:].indirect(T.l1[:]), T.bg[:], A.add), ["st", "l1", "bg"], ["bh"])
+
+    K0, K1 = T.psK0, T.psK1
 
     def meet(t, dst):
-        th, ck = 8.0 + t, 12.0 + t
-        X = 392 * t
+        th = 8.0 + t
+        X = 384 * t
+        last = t == RO - 1
         ts(T.bl[:], T.bh[:], 31, None, A.bitwise_and, None, ["bh"], ["bl"])
         ts(T.bk[:], T.bh[:], 114688, None, A.bitwise_and, None, ["bh"], ["bk"])
-        ts(T.bn[:], T.bl[:], th, BIG, A.is_ge, A.mult, ["bl"], ["bn"])
-        tt(T.bv[:], T.bk[:], T.bn[:], A.is_le, ["bk", "bn"], ["bv"])
-        tt(T.bp[:], T.bg[:], T.bv[:], A.mult, ["bg", "bv"], ["bp"])
-        tt(T.di[:], T.bp[:], T.psV[:, 256:384], A.subtract, ["bp", "psV"], ["di"])
-        act(T.dq[:], T.di[:], F.Square, ["di"], ["dq"], scale=1.0 / 1024)
-        if t < RO - 1:
-            vc(T.p16[:, 2:3], T.psC[:, 136:137], ["psC"], ["ai"])
-            ts(T.p16[:, 3:4], T.p16[:, 2:3], 31, None, A.bitwise_and, None, ["ai"], ["aj"])
-            ts(T.sa[:, 4 * t:4 * t + 1], T.p16[:, 3:4], -0.375, None, A.add, None, ["aj"], ["sa%d" % t])
-            send(dst, T.la[:, 4 * t:4 * t + 4], T.sa[:, 4 * t:4 * t + 4], ["sa", "sa%d" % t], "ra%d" % t)
-        tt(T.gb[:], T.bg[:], T.bn[:], A.mult, ["bg", "bn"], ["gb"])
-        ts(T.t1[:], T.bl[:], 16.0, None, A.is_ge, None, ["bl"], ["t1"])
-        ts(T.bq[:], T.bl[:], -1.0, ck, A.mult, A.add, ["bl"], ["bq"])
-        tt(T.bm[:], T.bl[:], T.ti[:], A.is_lt, ["bl", "ti"], ["bm"])
-        tt(T.t1b[:], T.t1[:], T.psV[:, 128:256], A.mult, ["t1", "psV"], ["t1b"])
-        tt(T.t2[:], T.bq[:], T.bm[:], A.mult, ["bq", "bm"], ["t2"])
-        tt(T.t1c[:], T.t1b[:], T.psV[:, 0:128], A.add, ["t1b", "psV"], ["t1c"])
-        tt(T.t2b[:], T.t2[:], T.bp[:], A.add, ["t2", "bp"], ["t2b"])
-        ts(T.ebz[:], T.bp[:], 0.0, 1.0 / BIG, A.is_equal, A.mult, ["bp"], ["ebz"])
-        tt(T.mx[:], T.t1c[:], T.t2b[:], A.max, ["t1c", "t2b"], ["mx"])
-        tt(T.x2[:, 0:128], T.ebz[:], T.psV[:, 384:512], A.mult, ["ebz", "psV"], ["x2"])
-        ts(T.sm[:], T.dq[:], 1.0, None, A.is_lt, None, ["dq"], ["sm"])
-        tt(T.x2[:, 128:256], T.x2[:, 0:128], T.bp[:], A.max, ["x2", "bp"], ["x2b"])
-        tt(T.pp[:], T.sm[:], T.mx[:], A.mult, ["sm", "mx"], ["pp"])
-        tt(T.w2[:], T.psC[:, 128:136], T.dl2[:], A.mult, ["psC", "dl2"], ["w2"])
-        tt(T.sx[:, X:X + 128], T.x2[:, 128:256], T.pp[:], A.max, ["x2b", "pp"], ["nb%d" % t])
+        ts(K0[:, 0:128], T.bl[:], th, BIG, A.is_ge, A.mult, ["bl"], ["psK0:bn"])
+        ts(K1[:, 0:128], T.bl[:], 16.0, None, A.is_ge, None, ["bl"], ["psK1:0"])
+        tt(K0[:, 128:256], T.bk[:], K0[:, 0:128], A.is_le, ["bk", "psK0:bn"], ["psK0:bv"])
+        tt(T.bs[:], T.bl[:], K0[:, 0:128], A.add, ["bl", "psK0:bn"], ["bs"])
+        act(T.bd2[:], T.bs[:], F.Relu, ["bs"], ["bd2"], bias=b_ck[t], scale=-1.0)
+        tt(T.bp[:], T.bg[:], K0[:, 128:256], A.mult, ["bg", "psK0:bv"], ["bp"])
+        ts(T.win[:], T.psC[:, 0:128], 0.5, None, A.is_lt, None, ["psC"], ["win"])
+        tt(T.di[:], T.bp[:], T.psG[:, 384:512], A.subtract, ["bp", "psG:c"], ["di"])
+        act(T.dq[:], T.di[:], F.Square, ["di"], ["dq"], bias=b_sq, scale=1.0 / 1024)
+        act(T.sg[:], T.dq[:], F.Sign, ["dq"], ["sg"], bias=b_one, scale=-1.0)
+        act(T.ebz[:], T.bp[:], F.Relu, ["bp"], ["ebz"], bias=b_ea, scale=-1.0 / BIG)
+        for s in range(16):
+            mm(T.psC[:, 128:136], T.zl[:, 15 - s:143 - s], T.win[:, s:128:16], s == 0, s == 15, ["zl", "win"], ["psC:l"])
+        if not last:
+            op("A", lambda: a.activation(T.wj[:], T.win[:], F.Copy, accum_out=T.pcol[:, 9:10]), ["win"], ["wj", "ca"])
+            act(T.cab[:, 0:1], T.pcol[:, 9:10], F.Copy, ["ca"], ["cab"])
+            mm(T.psC[:, 136:137], T.one16[:], T.cab[:, 0:1], True, True, ["one16", "cab"], ["psC:a"])
+        tt(K0[:, 256:384], T.bg[:], K0[:, 0:128], A.mult, ["bg", "psK0:bn"], ["psK0:gb"])
+        tt(K1[:, 128:256], K1[:, 0:128], T.ad[:], A.mult, ["psK1:0", "ad"], ["psK1:1"])
+        tt(K1[:, 256:384], T.bd2[:], T.psV[:, 256:384], A.mult, ["bd2", "psV:ia"], ["psK1:2"])
+        tt(K1[:, 0:128], K1[:, 128:256], T.ap[:], A.add, ["psK1:1", "ap"], ["psK1:3"])
+        tt(T.t2b[:], K1[:, 256:384], T.bp[:], A.add, ["psK1:2", "bp"], ["t2b"])
+
+        def a_new():
+            tt(K0[:, 384:512], K0[:, 256:384], T.ea[:], A.mult, ["psK0:gb", "ea"], ["psK0:x"])
+            tt(K0[:, 0:128], K0[:, 384:512], T.ap[:], A.max, ["psK0:x", "ap"], ["psK0:y"])
+            tt(K0[:, 128:256], K0[:, 0:128], T.pp[:], A.max, ["psK0:y", "pp"], ["psK0:z"])
+            tt(T.d2[:], K0[:, 128:256], T.lo[:, 256 * t:256 * t + 128], A.subtract, ["psK0:z", "lo%d" % t], ["d2"])
+            tt(K0[:, 256:384], T.d2[:], T.win[:], A.mult, ["d2", "win"], ["psK0:w"])
+            tt(T.sx[:, X + 128:X + 256], K0[:, 256:384], T.lo[:, 256 * t:256 * t + 128], A.add, ["psK0:w", "lo%d" % t], ["na%d" % t])
+
+        tt(K1[:, 128:256], T.t2b[:], K1[:, 0:128], A.max, ["t2b", "psK1:3"], ["psK1:4"])
+        tt(K1[:, 256:384], T.ebz[:], T.psV[:, 384:512], A.mult, ["ebz", "psV:ga"], ["psK1:5"])
+        tt(T.pp[:], K1[:, 128:256], T.sg[:], A.mult, ["psK1:4", "sg"], ["pp"])
+        if last:
+            a_new()
+            send(dst, T.ln[:, 256 * t:256 * t + 128], T.sx[:, X + 128:X + 256], ["na%d" % t], "rn%d" % t)
+        tt(K1[:, 384:512], K1[:, 256:384], T.bp[:], A.max, ["psK1:5", "bp"], ["psK1:6"])
+        tt(T.w2[:], T.psC[:, 128:136], T.dl2[:], A.mult, ["psC:l", "dl2"], ["w2"])
+        tt(T.sx[:, X:X + 128], K1[:, 384:512], T.pp[:], A.max, ["psK1:6", "pp"], ["nb%d" % t])
         tt(T.w2b[:], T.w2[:], T.dum[:], A.add, ["w2", "dum"], ["w2b"])
-        tt(T.x1[:, 0:128], T.gb[:], T.ea[:], A.mult, ["gb", "ea"], ["x1"])
+        if not last:
+            vc(T.p16[:, 2:3], T.psC[:, 136:137], ["psC:a"], ["ai"])
         vc(T.l2[:, 8 * t:8 * t + 8], T.w2b[:], ["w2b"], ["l2%d" % t])
-        if t < RO - 1:
-            scatter("raw", T.l2[:, 8 * t:8 * t + 8], T.sx[:, X:X + 128], ["l2%d" % t, "nb%d" % t], ["raw"])
-        tt(T.x1[:, 128:256], T.x1[:, 0:128], T.psV[:, 0:128], A.max, ["x1", "psV"], ["x1b"])
-        tt(T.w3[:], T.psC[:, 128:136], T.dl3[:, 8 * t:8 * t + 8], A.mult, ["psC", "dl3"], ["w3"])
-        tt(T.sx[:, X + 128:X + 256], T.x1[:, 128:256], T.pp[:], A.max, ["x1b", "pp"], ["na%d" % t])
-        o = X + 384 if t < RO - 1 else X + 256
-        tt(T.sx[:, o:o + 8], T.w3[:], T.dum[:], A.add, ["w3", "dum"], ["nl%d" % t])
-        if t == RO - 1:
-            send(dst, T.ln[:, 264 * t:264 * t + 136], T.sx[:, X + 128:X + 264], ["na%d" % t, "nl%d" % t], "rn%d" % t)
+        if last:
             return
-        z = slice(X, X + 256)
-        ts(T.cf1[:, 0:256], T.sx[:, z], -1024.5, MB, A.add, A.add, ["nb%d" % t, "na%d" % t], ["cf1"])
-        act(T.cf2[:, 0:256], T.sx[:, z], F.Identity, ["nb%d" % t, "na%d" % t], ["cf2"], bias=T.bcol[:, 0:1])
-        act(T.psG[:, 0:256], T.cf1[:, 0:256], F.Identity, ["cf1"], ["psG"], bias=T.bcol[:, 1:2], scale=0.0625)
-        act(T.cf2[:, 0:256], T.cf2[:, 0:256], F.Identity, ["cf2"], ["cf2"], bias=T.bcol[:, 2:3], scale=0.0625)
+        ts(T.p16[:, 3:4], T.p16[:, 2:3], 31, None, A.bitwise_and, None, ["ai"], ["aj"])
+        scatter("raw", T.l2[:, 8 * t:8 * t + 8], T.sx[:, X:X + 128], ["l2%d" % t, "nb%d" % t])
+        ts(T.sa[:, 4 * t:4 * t + 1], T.p16[:, 3:4], -0.375, None, A.add, None, ["aj", "sa"], ["sa%d" % t])
+        send(dst, T.la[:, 4 * t:4 * t + 4], T.sa[:, 4 * t:4 * t + 4], ["sa", "sa%d" % t], "ra%d" % t)
+        meet_rest.append(a_new)
+
+    meet_rest = []
+
+    def new_parts(t):
+        X = 384 * t
+        code_parts(T.sx[:, X:X + 256], ["nb%d" % t, "na%d" % t], T.c1[:], T.c2[:], "n", T.psG[:, 0:256])
 
     def finish(t, dst):
-        X = 392 * t
-        tt(T.nbc[:, 128 * t:128 * t + 128], T.psG[:, 0:128], T.cf2[:, 0:128], A.add, ["psG", "cf2"], ["nbc%d" % t])
-        tt(T.sx[:, X + 256:X + 384], T.psG[:, 128:256], T.cf2[:, 128:256], A.add, ["psG", "cf2"], ["nc%d" % t])
-        scatter("cod", T.l2[:, 8 * t:8 * t + 8], T.nbc[:, 128 * t:128 * t + 128], ["l2%d" % t, "nbc%d" % t], ["code"])
-        send(dst, T.ln[:, 264 * t:264 * t + 264], T.sx[:, X + 128:X + 392], ["na%d" % t, "nc%d" % t, "nl%d" % t], "rn%d" % t)
+        X = 384 * t
+        tt(T.sx[:, X + 256:X + 384], T.psG[:, 128:256], T.c2[:, 128:256], A.add, ["psG:n", "n2"], ["nc%d" % t])
+        tt(T.nbc[:, 128 * t:128 * t + 128], T.psG[:, 0:128], T.c2[:, 0:128], A.add, ["psG:n", "n2"], ["nbc%d" % t])
+        send(dst, T.ln[:, 256 * t:256 * t + 256], T.sx[:, X + 128:X + 384], ["na%d" % t, "nc%d" % t], "rn%d" % t)
+
+    def back_scalar(t):
+        o = 256 * t
+        lk = "ln%d" % t
+        act(T.raw[:, t:2048:16], T.ln[:, o:o + 128], F.Copy, [lk], ["raw"])
+        if t < RO - 1:
+            act(T.cod[:, t:2048:16], T.ln[:, o + 128:o + 256], F.Copy, [lk], ["cod"])
 
     def back(t):
-        o = 264 * t
-        X = 392 * t
-        last = t == RO - 1
-        lo = o + (128 if last else 256)
-        lk = "ln%d" % t
-        l3, l2 = T.l3[:, 8 * t:8 * t + 8], T.l2[:, 8 * t:8 * t + 8]
-        vc(l3, T.ln[:, lo:lo + 8], [lk], ["l3%d" % t])
-        scatter("raw", l3, T.ln[:, o:o + 128], [lk, "l3%d" % t], ["raw"])
-        if not last:
-            scatter("cod", l3, T.ln[:, o + 128:o + 256], [lk, "l3%d" % t], ["code"])
-            scatter("cod", l2, T.nbc[:, 128 * t:128 * t + 128], ["l2%d" % t, "nbc%d" % t], ["code"])
-        scatter("raw", l2, T.sx[:, X:X + 128], ["l2%d" % t, "nb%d" % t], ["raw"])
+        X = 384 * t
+        l2 = T.l2[:, 8 * t:8 * t + 8]
+        if t < RO - 1:
+            scatter("cod", l2, T.nbc[:, 128 * t:128 * t + 128], ["l2%d" % t, "nbc%d" % t, "cod"])
+        scatter("raw", l2, T.sx[:, X:X + 128], ["l2%d" % t, "nb%d" % t, "raw"])
 
+    b_mmb = T.pcol[:, 10:11]
+    b_sq = T.pcol[:, 11:12]
+    b_ck = [T.pcol[:, 12 + t:13 + t] for t in range(RO)]
     for t in range(RO):
         callee = T.cores[(rank + 1 + t % 7) % N]
         caller = T.cores[(rank - 1 - t % 7) % N]
         landed("lo%d" % t, "ro%d" % t)
-        landed("le%d0" % t, "re%d0" % t)
-        landed("le%d1" % t, "re%d1" % t)
+        landed("le%d" % t, "re%d" % t)
         landed("ln%d" % t, "rn%d" % t)
         if t < RO - 1:
             landed("la%d" % t, "ra%d" % t)
+        own_parts(t)
         lane_list(t)
-        if t == 0:
-            vc(T.pcol[:, 6:7], T.wti[:, 0:1], ["wti"], ["wcol"])
-            vc(T.pcol[:, 7:8], T.kpi[:, 0:1], ["kpi"], ["kcol"])
-            ts(T.wblk[:], T.bd[:], T.pcol[:, 6:7], None, A.mult, None, ["bd", "wcol"], ["wblk"])
-            first_table()
-            ts(T.z[:], T.z2[:], 32768.0, None, A.mult, None, ["z2"], ["z"])
-            ts(T.iz0[:], T.iz[:], T.pcol[:, 1:2], None, A.mult, None, ["iz", "pc1"], ["iz0"])
-            ts(T.iz1[:], T.iz[:], T.pcol[:, 2:3], None, A.mult, None, ["iz", "pc2"], ["iz1"])
-            ts(T.sb[:], T.bd[:], T.pcol[:, 4:5], None, A.mult, None, ["bd", "pc4"], ["sb"])
-        feat_act(0)
-        feat_act(1)
-        feat_vec(0)
+        features()
+        if t:
+            meet_rest.pop()()
+            new_parts(t - 1)
+        own_send(t, callee)
+        scans(t)
         if t:
             finish(t - 1, prev)
-        own_send(t, callee)
-        cand(t, 0, callee)
-        feat_vec(1)
-        cand(t, 1, callee)
+        cand(t, callee)
+        if t == 0:
+            ms(b_mmb, -MB, ["bx0"])
+            ms(b_sq, -1024.5 / 1024, ["bx1"])
+            for i in range(RO):
+                ms(b_ck[i], 12.0 + i, ["bx2"])
+            ts(T.z[:], T.z2[:], 32768.0, None, A.mult, None, ["z2"], ["z"])
+            first_raw()
+            wait("A", [wr[k][0][1] for k in ("bx0", "bx1", "bx2")])
         expand(t, 0)
         expand(t, 1)
         own_side(t)
-        if t:
+        if t == 0:
+            first_cod()
+        else:
+            back_scalar(t - 1)
             back(t - 1)
         score(t)
+        own_side_scalar(t)
         partner(t)
         meet(t, caller)
         prev = caller
+    back_scalar(RO - 1)
     back(RO - 1)
     dma("S", T.yent[:, 0:1024], T.raw[:, 0:1024], ["raw"], [], "dy")
     dma("A", T.yent[:, 1024:2048], T.raw[:, 1024:2048], ["raw"], [], "dy")
     for s in tot:
         wait("G", [(s, tot[s], {})])
-
-
-SCRATCH["bcol"] = ("sbuf", [128, 4], "float32")

@@ -7,15 +7,16 @@ MB = M0 * 2048.0
 BIG = 1048576.0
 W = 2048 + 128
 NE = 8
-VS = 40
+M16 = M0 * 16.0
+VS, VS0 = 40, 16
 
 _F, _B, _I, _H, _U = "float32", "bfloat16", "int32", "float16", "uint16"
 SCRATCH = {}
 for _n, _w, _d in [
         ("ents", 2048, _I), ("raw", W, _F), ("cod", W, _F), ("st", 2048, _F), ("fw", 4112, _B), ("cf1", 2048, _F), ("cf2", 2048, _F),
-        ("wti", 4, _I), ("kpi", 4, _I), ("bcol", 8, _F),
+        ("wti", 4, _I), ("kpi", 4, _I), ("bcol", 16, _F),
         ("ones", 160, _B), ("one16", 128, _B), ("bd0", 128, _B), ("bd", 128, _B), ("z0", 144, _B), ("z1", 144, _B), ("z2", 144, _B),
-        ("z", 144, _B), ("zl", 144, _B), ("iz", 160, _B), ("iz0", 160, _H), ("iz1", 160, _H), ("sb", 128, _H), ("wblk", 128, _B),
+        ("z", 144, _B), ("zl", 144, _B), ("zn", 144, _B), ("iz", 160, _B), ("iz0", 160, _H), ("iz1", 160, _H), ("sb", 128, _H), ("wblk", 128, _B),
         ("fm", 2048, _B), ("cli", 128, _I), ("cl", 128, _U), ("pi", 4, _I), ("pcol", 16, _F), ("p16", 4, _I), ("ii", 8, _I),
         ("dum", 8, _F), ("dmc", 8, _F), ("ji", 16, _I), ("sti", 64, _I), ("stj", 64, _I),
         ("i1", 128, _I), ("i2", 128, _I), ("i3", 128, _I), ("lst", 128, _U), ("fg", 2048, _B), ("fs", 2048, _B),
@@ -31,11 +32,14 @@ for _n, _w, _d in [
         ("bg", 128, _F), ("bh", 128, _I), ("bl", 128, _I), ("bk", 128, _I), ("bs", 128, _F), ("bp", 128, _F), ("di", 128, _F),
         ("dq", 128, _F), ("sg", 128, _F), ("ebz", 128, _F), ("bd2", 128, _F), ("t2b", 128, _F), ("pp", 128, _F), ("d2", 128, _F)]:
     SCRATCH[_n] = ("sbuf", [128, _w], _d)
-SCRATCH["tri"] = ("sbuf", [128, 8, 16], _B)
-SCRATCH["eq"] = ("sbuf", [128, 8, 144], _B)
+for _n, _w, _d in [("idf", 128, _F), ("trb", 512, _B), ("big", 1024, _B), ("pb", 1024, _B), ("pc", 1024, _H), ("nc", 1024, _H), ("wg", 240, _B),
+                   ("sq", 512, _B), ("eq", 1024, _B), ("aa", 4, _F)]:
+    SCRATCH[_n] = ("sbuf", [128, _w], _d)
+for _n in ("ji", "sb", "key"):
+    SCRATCH.pop(_n)
 for _n in ("psU", "psK0", "psK1", "psL", "psR", "psC", "psG", "psV"):
     SCRATCH[_n] = ("psum", [128, 512], _F)
-SEMAPHORES = (["sV", "sA", "sP", "sG", "dent", "dsm", "dfe", "dst", "dy", "loc"]
+SEMAPHORES = (["sV", "sA", "sP", "sG", "dent", "dsm", "dfe", "dy", "loc"]
               + ["%s%d" % (k, t) for k in ("ro", "re", "rn", "ra") for t in range(RO)])
 
 
@@ -162,6 +166,7 @@ def rank_program(g, core, T, topo):
     joined("fw", "dfe")
 
     ms(T.ones[:], 1.0, ["ones"])
+    ms(T.big[:], 4096.0, ["big"])
     op("G", lambda: g.iota(T.sti[:], [[37, 64]], 0, 0), [], ["sti"])
     op("G", lambda: g.iota(T.pi[:, 0:1], [[1, 1]], 0, 1), [], ["pi"])
     op("G", lambda: g.affine_select(T.bd0[:], T.ones[:, 0:128], [[-16, 8], [0, 16]], A.is_ge, 0.0, 0, 1), ["ones"], ["bd0"])
@@ -172,27 +177,28 @@ def rank_program(g, core, T, topo):
     op("G", lambda: g.affine_select(T.z2[:], T.z1[:], [[0, 9], [1, 16]], A.is_equal, 0.0, -15, 0), ["z1"], ["z2"])
     op("G", lambda: g.affine_select(T.iz[:], T.ones[:], [[-1, 160]], A.is_equal, 0.0, 16, 1), ["ones"], ["iz"])
     op("G", lambda: g.iota(T.ii[:], [[16, 8]], 2048, 0), [], ["ii"])
-    op("G", lambda: g.iota(T.ji[:], [[1, 16]], 0, 0), [], ["ji"])
-    b_w, b_f, b_w1, b_mb, b_g, b_64, b_ea = [bias(c) for c in (-8.5, M0, -1024.5, MB, -MB / 16, -64.0, 1.0 / BIG)]
-    b_one = bias(1.0)
+    op("G", lambda: g.affine_select(T.trb[:], T.big[:, 0:512], [[0, 4], [-1, 128]], A.is_ge, 0.0, 0, 1), ["big"], ["trb"])
+    op("G", lambda: g.affine_select(T.pb[:], T.big[:], [[-16, 8], [0, 128]], A.is_equal, 0.0, -15, 1), ["big"], ["pb"])
+    ts(T.stj[:], T.sti[:], 63, None, A.bitwise_and, None, ["sti"], ["stj"])
+    ts(T.st[:, 0:64], T.stj[:], 2048.0, -17.0, A.mult, A.add, ["stj"], ["st"])
+    n = 64
+    while n < 2048:
+        act(T.st[:, n:2 * n], T.st[:, 0:n], F.Copy, ["st"], ["st"])
+        n *= 2
+    b_w, b_f, b_w1, b_mb, b_mmb, b_64, b_ea, b_one, b_15, b_m32 = [
+        bias(c) for c in (-8.5, M16, -1024.5, MB, -MB, -64.0, 1.0 / BIG, 1.0, -15.5, M0 * 32)]
     wait("A", [wr["bc%d" % i][0][1] for i in range(len(BC))])
     ms(T.fm[:], 1.0, ["fm"])
     op("V", lambda: v.memset(T.fm[:, 0:2048:16], 0.0), ["fm"], ["fm"])
     ms(T.fw[:, 4096:4112], 0.0, ["fwz"])
-    ms(T.pcol[:, 8:9], -0.375, ["acol"])
-    ts(T.stj[:], T.sti[:], 63, None, A.bitwise_and, None, ["sti"], ["stj"])
+    ms(T.pcol[:, 8:9], 0.0, ["acol"])
     ts(T.p16[:, 0:1], T.pi[:, 0:1], 15, None, A.bitwise_and, None, ["pi"], ["p16"])
     ts(T.p16[:, 1:2], T.pi[:, 0:1], 16, None, A.bitwise_and, None, ["pi"], ["p16b"])
-    ts(T.st[:, 0:64], T.stj[:], 2048.0, -17.0, A.mult, A.add, ["stj"], ["st"])
     ts(T.pcol[:, 3:4], T.p16[:, 0:1], -2048.0, 15 * 2048 - 1023.5, A.mult, A.add, ["p16"], ["pc3"])
     vc(T.cl[:], T.cli[:], ["cli"], ["cl"])
     vc(T.pcol[:, 6:7], T.wti[:, 0:1], ["wti"], ["wcol"])
     vc(T.pcol[:, 7:8], T.kpi[:, 0:1], ["kpi"], ["kcol"])
     ts(T.wblk[:], T.bd[:], T.pcol[:, 6:7], None, A.mult, None, ["bd", "wcol"], ["wblk"])
-    n = 64
-    while n < 2048:
-        dma("S", T.st[:, n:2 * n], T.st[:, 0:n], ["st"], ["st"], "dst")
-        n *= 2
 
     def more_constants():
         ms(T.one16[:], 0.0625, ["one16"])
@@ -200,30 +206,31 @@ def rank_program(g, core, T, topo):
         vc(T.pcol[:, 0:1], T.p16[:, 0:1], ["p16"], ["pc0"])
         ts(T.pcol[:, 1:2], T.p16[:, 1:2], 0.0, None, A.is_equal, None, ["p16b"], ["pc1"])
         ts(T.pcol[:, 2:3], T.p16[:, 1:2], 0.0, None, A.is_gt, None, ["p16b"], ["pc2"])
-        ts(T.pcol[:, 4:5], T.p16[:, 0:1], 15.0, None, A.is_equal, None, ["p16"], ["pc4"])
+        ts(T.pc[:], T.pb[:], 2.0 ** -12, None, A.mult, None, ["pb"], ["pc"])
+        ts(T.nc[:], T.pb[:], -2.0 ** -12, None, A.mult, None, ["pb"], ["nc"])
+        ms(T.wg[:], 0.0, ["wg0"])
+        op("V", lambda: v.memset(T.wg[:, 112:128], 1.0), ["wg0"], ["wg"])
         ts(T.zl[:], T.z2[:], 0.0625, None, A.mult, None, ["z2"], ["zl"])
         ts(T.iz0[:], T.iz[:], T.pcol[:, 1:2], None, A.mult, None, ["iz", "pc1"], ["iz0"])
         ts(T.iz1[:], T.iz[:], T.pcol[:, 2:3], None, A.mult, None, ["iz", "pc2"], ["iz1"])
-        ts(T.sb[:], T.bd[:], T.pcol[:, 4:5], None, A.mult, None, ["bd", "pc4"], ["sb"])
         ts(T.dum[:], T.ii[:], T.pcol[:, 0:1], None, A.add, None, ["ii", "pc0"], ["dum"])
         yield
-        for c in range(8):
-            ts(T.tri[:, c, 0:16], T.ji[:], T.pcol[:, 0:1], None, A.is_gt, None, ["ji", "pc0"], ["tri"])
-        yield
         ts(T.dmc[:], T.dum[:], -1023.5, None, A.add, None, ["dum"], ["dmc"])
+        for i in range(4):
+            s = slice(512 * i, 512 * i + 512)
+            vc(T.raw[:, s], T.ents[:, s], ["ents"], ["raw"])
+            if i % 2:
+                yield
 
     banks = ["psK0", "psK1", "psR", "psC"]
 
-    def first_raw():
-        for i in range(4):
+    def first_parts(blocks):
+        for i in blocks:
             s = slice(512 * i, 512 * i + 512)
             k = "@%d" % i
-            vc(T.raw[:, s], T.ents[:, s], ["ents"], ["raw" + k])
-            act(T.cf2[:, s], T.raw[:, s], F.Identity, ["raw" + k], ["cf2" + k], bias=b_w)
-            act(T.cf2[:, s], T.cf2[:, s], F.Identity, ["cf2" + k], ["cf2" + k], bias=b_f, scale=0.0625)
             ts(T.cf1[:, s], T.ents[:, s], -1024.5, MB, A.add, A.add, ["ents"], ["cf1" + k])
-            act(T[banks[i]][:], T.cf1[:, s], F.Identity, ["cf1" + k], [banks[i]], bias=b_g, scale=0.0625)
-        wr["raw"] = list(wr["raw@3"])
+            act(T[banks[i]][:], T.cf1[:, s], F.Identity, ["cf1" + k], [banks[i]], bias=b_mmb)
+            ts(T.cf2[:, s], T.ents[:, s], -8.5, M16, A.add, A.add, ["ents"], ["cf2" + k])
 
     def first_cod():
         for i in range(4):
@@ -233,9 +240,9 @@ def rank_program(g, core, T, topo):
     def code_parts(src, sk, t1, t2, k, ps):
         act(t2, src, F.Identity, sk, [k + "2"], bias=b_w)
         act(t1, src, F.Identity, sk, [k + "1"], bias=b_w1)
-        act(t2, t2, F.Identity, [k + "2"], [k + "2"], bias=b_f, scale=0.0625)
+        act(t2, t2, F.Identity, [k + "2"], [k + "2"], bias=b_f)
         act(t1, t1, F.Identity, [k + "1"], [k + "1"], bias=b_mb)
-        act(ps, t1, F.Identity, [k + "1"], [("psG:" if k == "n" else "psL:") + k], bias=b_g, scale=0.0625)
+        act(ps, t1, F.Identity, [k + "1"], [("psG:" if k == "n" else "psL:") + k], bias=b_mmb)
 
     def lane_list(t):
         src, sk = (T.ents, "ents") if t == 0 else (T.raw, "raw")
@@ -259,13 +266,13 @@ def rank_program(g, core, T, topo):
         tt(T.so[:, o + 128:o + 256], T.psL[:, 256:384], T.o2[:], A.add, ["psL:o", "o2"], ["soc%d" % t])
         send(dst, T.lo[:, o:o + 256], T.so[:, o:o + 256], ["so%d" % t, "soc%d" % t], "ro%d" % t)
 
-    def features():
+    def features(vs):
         rk = ["lst", "fw", "fwz"]
-        op("A", lambda: a.activation(T.fg[:, 16 * VS:2048], T.fw[:].indirect(T.lst[:, VS:128]), F.Copy), rk, ["fgA"])
-        op("V", lambda: v.tensor_copy(T.fg[:, 0:16 * VS], T.fw[:].indirect(T.lst[:, 0:VS])), rk, ["fgV"])
+        op("A", lambda: a.activation(T.fg[:, 16 * vs:2048], T.fw[:].indirect(T.lst[:, vs:128]), F.Copy), rk, ["fgA"])
+        op("V", lambda: v.tensor_copy(T.fg[:, 0:16 * vs], T.fw[:].indirect(T.lst[:, 0:vs])), rk, ["fgV"])
 
-    def scans(t):
-        for n0, n1, k in ((0, VS, "V"), (VS, 128, "A")):
+    def scans(vs):
+        for n0, n1, k in ((0, vs, "V"), (vs, 128, "A")):
             c = slice(16 * n0, 16 * n1)
             op("V", lambda: v.tensor_tensor_scan(T.fs[:, c], T.fm[:, c], T.fg[:, c], 0.0, A.mult, A.max), ["fm", "fg" + k], ["fs" + k])
         mm(T.psU[:, 0:128], T.wblk[:], T.fs[:, 15:2048:16], True, True, ["wblk", "fsV", "fsA"], ["psU"])
@@ -277,7 +284,7 @@ def rank_program(g, core, T, topo):
         ts(T.u2[:], T.u1[:], 4095, None, A.bitwise_and, None, ["u1"], ["u2"])
         ts(T.psV[:, 0:128], T.u2[:], 0.03125, T.pcol[:, 7:8], A.mult, A.add, ["u2", "kcol"], ["psV:1"])
         tt(T.u4[:], T.psV[:, 0:128], T.u2[:], A.mult, ["psV:1", "u2"], ["u4"])
-        ts(T.u5[:], T.u4[:], ac, None, A.add, None, ["u4", ak], ["u5"])
+        ts(T.u5[:], T.u4[:], ac, -0.375, A.add, A.add, ["u4", ak], ["u5"])
         ts(T.u6[:], T.u5[:], 2047, None, A.bitwise_and, None, ["u5"], ["u6"])
         vc(T.se[:, o:o + 128], T.u6[:], ["u6"], ["se%d" % t])
         send(dst, T.le[:, o:o + 128], T.se[:, o:o + 128], ["se%d" % t], "re%d" % t)
@@ -316,8 +323,7 @@ def rank_program(g, core, T, topo):
     todo = [more_constants()]
 
     def fill():
-        if todo:
-            next(todo[0], None)
+        return next(todo[0], 1) is None
 
     def score(t):
         def gat(i):
@@ -325,42 +331,57 @@ def rank_program(g, core, T, topo):
             o = 128 * t
             op("V", lambda: v.tensor_tensor(T.dd[:, c], T.cod[:, 0:2048].indirect(T.le[:, o + CH[i]:o + CH[i + 1]]), T.ox[:, c], A.subtract),
                ["cod", "le%d" % t, "ox%d" % (i // 2)], ["dd%d" % i])
-            act(T.da[:, c], T.dd[:, c], F.Abs, ["dd%d" % i], ["da%d" % i])
-            act(T.db[:, c], T.da[:, c], F.Abs, ["da%d" % i], ["db%d" % i], bias=b_64)
+            act(T.da[:, c], T.dd[:, c], F.Abs, ["dd%d" % i], ["da%d" % i], scale=0.0625)
+            if i > 1:
+                act(T.db[:, c], T.da[:, c], F.Abs, ["da%d" % i], ["db%d" % i], bias=b_64)
 
         def thr(i):
             c = slice(16 * CH[i], 16 * CH[i + 1])
-            ts(T.mt[:, c], T.db[:, c], 63.75, None, A.is_lt, None, ["db%d" % i], ["mt%d" % i])
+            if i > 1:
+                ts(T.mt[:, c], T.db[:, c], 63.75, None, A.is_lt, None, ["db%d" % i], ["mt%d" % i])
+            else:
+                ts(T.mt[:, c], T.da[:, c], 127.5, None, A.is_lt, None, ["da%d" % i], ["mt%d" % i])
+
+        def same(i):
+            c = slice(16 * CH[i], 16 * CH[i + 1])
+            ts(T.db[:, c], T.da[:, c], 0.5, None, A.is_lt, None, ["da%d" % i], ["db%d" % i])
 
         def add(h):
-            k = "psK%d" % h
-            for m in range(16):
-                mm(T[k][:, 0:64], T.z[:, 15 - m:143 - m], T.mt[:, 1024 * h + m:1024 * h + 1024:16], m == 0, m == 15,
-                   ["z", "mt%d" % (2 * h), "mt%d" % (2 * h + 1)], [k + ":k"])
-
-        def keyh(h):
+            k = "psK0:k%d" % h
             s = slice(64 * h, 64 * h + 64)
-            tt(T.key[:, s], T["psK%d" % h][:, 0:64], T.eb[:, s], A.add, ["psK%d:k" % h, "eb"], ["key%d" % h])
+            mm(T.psK0[:, s], T.idf[:], T.eb[:, s], True, False, ["idf", "eb"], [k])
+            for m in range(16):
+                mm(T.psK0[:, s], T.z[:, 15 - m:143 - m], T.mt[:, 1024 * h + m:1024 * h + 1024:16], False, m == 15 and h == 1,
+                   ["z", "mt%d" % (2 * h), "mt%d" % (2 * h + 1)], [k])
+
+        def sub():
+            for m in range(16):
+                mm(T.psK0[:, 0:64], T.zn[:, 15 - m:143 - m], T.db[:, m:1024:16], False, m == 15,
+                   ["zn", "db0", "db1"], ["psK0:k0"])
 
         gat(0)
         gat(1)
         ts(T.eb[:], T.le[:, 128 * t:128 * t + 128], T.pcol[:, 3:4], None, A.add, None, ["le%d" % t, "pc3"], ["eb"])
-        fill()
-        thr(0)
         gat(2)
+        thr(0)
         thr(1)
         add(0)
         gat(3)
+        same(0)
+        same(1)
+        sub()
+        fill()
         thr(2)
-        keyh(0)
         fill()
         thr(3)
         add(1)
-        fill()
-        keyh(1)
+        while fill():
+            pass
 
     def partner(t):
-        op("V", lambda: v.transpose(T.kt[:], T.key[:]), ["key0", "key1"], ["kt"])
+        for i, k in enumerate(("psU", "psR")):
+            mm(T[k][:], T.iz[:, 16:144], T.trb[:], True, False, ["iz", "trb"], [k + ":d"])
+        op("V", lambda: v.transpose(T.kt[:], T.psK0[:, 0:128]), ["psK0:k0", "psK0:k1"], ["kt"])
         op("V", lambda: v.tensor_tensor_scan(T.ks[:], T.fm[:, 0:128], T.kt[:], 0.0, A.mult, A.max), ["fm", "kt"], ["ks"])
         ts(T.psK1[:, 0:128], T.ks[:], MB, -MB, A.add, A.add, ["ks"], ["psK1:0"])
         tt(T.et[:], T.ks[:], T.psK1[:, 0:128], A.subtract, ["ks", "psK1:0"], ["et"])
@@ -370,16 +391,16 @@ def rank_program(g, core, T, topo):
                 mm(T.psL[:, h:8:2], T["iz%d" % h][:, b:b + 128], T.et[:, 16 * g2 + 15:128:32], g2 == 0, g2 == 1,
                    ["iz%d" % h, "et"], ["psL"])
         op("V", lambda: v.transpose(T.rt[:], T.et[:]), ["et"], ["rt"])
-        mm(T.psR[:, 0:128], T.sb[:], T.rt[:], True, True, ["sb", "rt"], ["psR"])
+        for i, k in enumerate(("psU", "psR")):
+            mm(T[k][:], T.rt[:], T.nc[:, 512 * i:512 * i + 512], False, False, ["rt", "nc"], [k + ":d"])
+            for b in range(4):
+                c = 512 * i + 128 * b
+                mm(T[k][:, 128 * b:128 * b + 128], T.pc[:, c:c + 128], T.rt[:], False, b == 3, ["rt", "pc"], [k + ":d"])
+        act(T.sq[:], T.psU[:], F.Square, ["psU:d"], ["sq"])
+        act(T.eq[:, 0:512], T.sq[:], F.Relu, ["sq"], ["eq0"], bias=b_one, scale=-1.0)
         ts(T.l1[:], T.psL[:, 0:8], 1023.5, None, A.add, None, ["psL"], ["l1"])
         tt(T.dl2[:], T.psL[:, 0:8], T.dmc[:], A.subtract, ["psL", "dmc"], ["dl2"])
-        for c in range(8):
-            op("V", lambda: v.tensor_scalar(T.eq[:, c, 0:128 - 16 * c], T.psR[:, 16 * c:128], T.psL[:, c:c + 1], None, A.is_equal),
-               ["psR", "psL"], ["eq"])
         op("V", lambda: v.tensor_copy(T.bg[:], T.raw[:, 0:2048].indirect(T.l1[:])), ["raw", "l1"], ["bg"])
-        tt(T.eq[:, :, 0:16], T.eq[:, :, 0:16], T.tri[:], A.mult, ["eq", "tri"], ["eq"])
-        for c in range(8):
-            mm(T.psC[:, 16 * c:128], T.bd[:], T.eq[:, c, 0:128 - 16 * c], c == 0, c == 7, ["bd", "eq"], ["psC"])
         op("V", lambda: v.tensor_tensor(T.bh[:], T.st[:].indirect(T.l1[:]), T.bg[:], A.add), ["st", "l1", "bg"], ["bh"])
 
     K0, K1 = T.psK0, T.psK1
@@ -396,51 +417,59 @@ def rank_program(g, core, T, topo):
         tt(T.bs[:], T.bl[:], K0[:, 0:128], A.add, ["bl", "psK0:bn"], ["bs"])
         act(T.bd2[:], T.bs[:], F.Relu, ["bs"], ["bd2"], bias=b_ck[t], scale=-1.0)
         tt(T.bp[:], T.bg[:], K0[:, 128:256], A.mult, ["bg", "psK0:bv"], ["bp"])
-        ts(T.win[:], T.psC[:, 0:128], 0.5, None, A.is_lt, None, ["psC"], ["win"])
+        ts(T.eq[:, 512:1024], T.psR[:], 0.0, None, A.is_equal, None, ["psR:d"], ["eq1"])
+        for c in range(8):
+            mm(T.psC[:, 0:128], T.wg[:, 112 - 16 * c:240 - 16 * c], T.eq[:, 128 * c:128 * c + 128], c == 0, c == 7,
+               ["wg", "eq%d" % (c // 4)], ["psC"])
         tt(T.di[:], T.bp[:], T.psG[:, 384:512], A.subtract, ["bp", "psG:c"], ["di"])
         act(T.dq[:], T.di[:], F.Square, ["di"], ["dq"], bias=b_sq, scale=1.0 / 1024)
         act(T.sg[:], T.dq[:], F.Sign, ["dq"], ["sg"], bias=b_one, scale=-1.0)
         act(T.ebz[:], T.bp[:], F.Relu, ["bp"], ["ebz"], bias=b_ea, scale=-1.0 / BIG)
+        act(T.win[:], T.psC[:, 0:128], F.Relu, ["psC"], ["win"], bias=b_one, scale=-1.0)
         for s in range(16):
             mm(T.psC[:, 128:136], T.zl[:, 15 - s:143 - s], T.win[:, s:128:16], s == 0, s == 15, ["zl", "win"], ["psC:l"])
         if not last:
             op("A", lambda: a.activation(T.wj[:], T.win[:], F.Copy, accum_out=T.pcol[:, 9:10]), ["win"], ["wj", "ca"])
             act(T.cab[:, 0:1], T.pcol[:, 9:10], F.Copy, ["ca"], ["cab"])
             mm(T.psC[:, 136:137], T.one16[:], T.cab[:, 0:1], True, True, ["one16", "cab"], ["psC:a"])
+            pa = T.psC[:, 136:137]
+            act(T.aa[:, 0:1], pa, F.Identity, ["psC:a"], ["aa0"], bias=b_15)
+            act(T.aa[:, 1:2], T.aa[:, 0:1], F.Identity, ["aa0"], ["aa1"], bias=b_m32)
+            act(T.aa[:, 2:3], T.aa[:, 1:2], F.Identity, ["aa1"], ["aa2"], bias=b_m32, scale=-1.0)
+            act(T.sa[:, 4 * t:4 * t + 1], pa, F.Identity, ["psC:a", "aa2", "sa"], ["sa%d" % t], bias=T.aa[:, 2:3])
+            send(dst, T.la[:, 4 * t:4 * t + 4], T.sa[:, 4 * t:4 * t + 4], ["sa", "sa%d" % t], "ra%d" % t)
         tt(K0[:, 256:384], T.bg[:], K0[:, 0:128], A.mult, ["bg", "psK0:bn"], ["psK0:gb"])
         tt(K1[:, 128:256], K1[:, 0:128], T.ad[:], A.mult, ["psK1:0", "ad"], ["psK1:1"])
         tt(K1[:, 256:384], T.bd2[:], T.psV[:, 256:384], A.mult, ["bd2", "psV:ia"], ["psK1:2"])
         tt(K1[:, 0:128], K1[:, 128:256], T.ap[:], A.add, ["psK1:1", "ap"], ["psK1:3"])
         tt(T.t2b[:], K1[:, 256:384], T.bp[:], A.add, ["psK1:2", "bp"], ["t2b"])
 
-        def a_new():
+        def a_new1():
             tt(K0[:, 384:512], K0[:, 256:384], T.ea[:], A.mult, ["psK0:gb", "ea"], ["psK0:x"])
             tt(K0[:, 0:128], K0[:, 384:512], T.ap[:], A.max, ["psK0:x", "ap"], ["psK0:y"])
             tt(K0[:, 128:256], K0[:, 0:128], T.pp[:], A.max, ["psK0:y", "pp"], ["psK0:z"])
             tt(T.d2[:], K0[:, 128:256], T.lo[:, 256 * t:256 * t + 128], A.subtract, ["psK0:z", "lo%d" % t], ["d2"])
+
+        def a_new2():
             tt(K0[:, 256:384], T.d2[:], T.win[:], A.mult, ["d2", "win"], ["psK0:w"])
             tt(T.sx[:, X + 128:X + 256], K0[:, 256:384], T.lo[:, 256 * t:256 * t + 128], A.add, ["psK0:w", "lo%d" % t], ["na%d" % t])
 
         tt(K1[:, 128:256], T.t2b[:], K1[:, 0:128], A.max, ["t2b", "psK1:3"], ["psK1:4"])
         tt(K1[:, 256:384], T.ebz[:], T.psV[:, 384:512], A.mult, ["ebz", "psV:ga"], ["psK1:5"])
         tt(T.pp[:], K1[:, 128:256], T.sg[:], A.mult, ["psK1:4", "sg"], ["pp"])
+        a_new1()
         if last:
-            a_new()
+            a_new2()
             send(dst, T.ln[:, 256 * t:256 * t + 128], T.sx[:, X + 128:X + 256], ["na%d" % t], "rn%d" % t)
         tt(K1[:, 384:512], K1[:, 256:384], T.bp[:], A.max, ["psK1:5", "bp"], ["psK1:6"])
         tt(T.w2[:], T.psC[:, 128:136], T.dl2[:], A.mult, ["psC:l", "dl2"], ["w2"])
         tt(T.sx[:, X:X + 128], K1[:, 384:512], T.pp[:], A.max, ["psK1:6", "pp"], ["nb%d" % t])
         tt(T.w2b[:], T.w2[:], T.dum[:], A.add, ["w2", "dum"], ["w2b"])
-        if not last:
-            vc(T.p16[:, 2:3], T.psC[:, 136:137], ["psC:a"], ["ai"])
         vc(T.l2[:, 8 * t:8 * t + 8], T.w2b[:], ["w2b"], ["l2%d" % t])
         if last:
             return
-        ts(T.p16[:, 3:4], T.p16[:, 2:3], 31, None, A.bitwise_and, None, ["ai"], ["aj"])
         scatter("raw", T.l2[:, 8 * t:8 * t + 8], T.sx[:, X:X + 128], ["l2%d" % t, "nb%d" % t])
-        ts(T.sa[:, 4 * t:4 * t + 1], T.p16[:, 3:4], -0.375, None, A.add, None, ["aj", "sa"], ["sa%d" % t])
-        send(dst, T.la[:, 4 * t:4 * t + 4], T.sa[:, 4 * t:4 * t + 4], ["sa", "sa%d" % t], "ra%d" % t)
-        meet_rest.append(a_new)
+        meet_rest.append(a_new2)
 
     meet_rest = []
 
@@ -468,7 +497,6 @@ def rank_program(g, core, T, topo):
             scatter("cod", l2, T.nbc[:, 128 * t:128 * t + 128], ["l2%d" % t, "nbc%d" % t, "cod"])
         scatter("raw", l2, T.sx[:, X:X + 128], ["l2%d" % t, "nb%d" % t, "raw"])
 
-    b_mmb = T.pcol[:, 10:11]
     b_sq = T.pcol[:, 11:12]
     b_ck = [T.pcol[:, 12 + t:13 + t] for t in range(RO)]
     for t in range(RO):
@@ -481,32 +509,36 @@ def rank_program(g, core, T, topo):
             landed("la%d" % t, "ra%d" % t)
         own_parts(t)
         lane_list(t)
-        features()
-        if t:
+        vs = VS if t else VS0
+        features(vs)
+        own_send(t, callee)
+        if t == 0:
+            first_parts((0, 1))
+        else:
             meet_rest.pop()()
             new_parts(t - 1)
-        own_send(t, callee)
-        scans(t)
+        scans(vs)
         if t:
             finish(t - 1, prev)
         cand(t, callee)
         if t == 0:
-            ms(b_mmb, -MB, ["bx0"])
+            first_parts((2, 3))
+            ts(T.z[:], T.z2[:], 32768.0, None, A.mult, None, ["z2"], ["z"])
+            vc(T.idf[:], T.iz[:, 16:144], ["iz"], ["idf"])
+            ts(T.zn[:], T.z2[:], -32768.0, None, A.mult, None, ["z2"], ["zn"])
             ms(b_sq, -1024.5 / 1024, ["bx1"])
             for i in range(RO):
                 ms(b_ck[i], 12.0 + i, ["bx2"])
-            ts(T.z[:], T.z2[:], 32768.0, None, A.mult, None, ["z2"], ["z"])
-            first_raw()
-            wait("A", [wr[k][0][1] for k in ("bx0", "bx1", "bx2")])
+            first_cod()
         expand(t, 0)
         expand(t, 1)
         own_side(t)
-        if t == 0:
-            first_cod()
-        else:
+        if t:
             back_scalar(t - 1)
             back(t - 1)
         score(t)
+        if t == 0:
+            wait("A", [wr[k][0][1] for k in ("bx1", "bx2")])
         own_side_scalar(t)
         partner(t)
         meet(t, caller)

from concourse.mybir import AluOpType, ActivationFunctionType

N = 8
RO = 4
M0 = 12582912.0
MB = M0 * 2048.0
BIG = 1048576.0
W = 2048 + 128
NE = 8
M16 = M0 * 16.0
VS, VS0 = 40, 16

_F, _B, _I, _H, _U = "float32", "bfloat16", "int32", "float16", "uint16"
SCRATCH = {}
for _n, _w, _d in [
        ("ents", 2048, _I), ("raw", W, _F), ("cod", W, _F), ("st", 2048, _F), ("fw", 4112, _B), ("cf1", 2048, _F), ("cf2", 2048, _F),
        ("wti", 4, _I), ("kpi", 4, _I), ("bcol", 16, _F),
        ("ones", 160, _B), ("one16", 128, _B), ("bd0", 128, _B), ("bd", 128, _B), ("z0", 144, _B), ("z1", 144, _B), ("z2", 144, _B),
        ("z", 144, _B), ("zl", 144, _B), ("zn", 144, _B), ("iz", 160, _B), ("iz0", 160, _H), ("iz1", 160, _H), ("sb", 128, _H), ("wblk", 128, _B),
        ("fm", 2048, _B), ("cli", 128, _I), ("cl", 128, _U), ("pi", 4, _I), ("pcol", 16, _F), ("p16", 4, _I), ("ii", 8, _I),
        ("dum", 8, _F), ("dmc", 8, _F), ("ji", 16, _I), ("sti", 64, _I), ("stj", 64, _I),
        ("i1", 128, _I), ("i2", 128, _I), ("i3", 128, _I), ("lst", 128, _U), ("fg", 2048, _B), ("fs", 2048, _B),
        ("u1", 128, _I), ("u2", 128, _I), ("u4", 128, _F), ("u5", 128, _I), ("u6", 128, _I),
        ("se", 512, _U), ("le", 512, _U), ("so", 1024, _F), ("lo", 1024, _F), ("sa", 16, _F), ("la", 16, _F),
        ("sx", 4 * 384, _F), ("ln", 4 * 256, _F), ("nbc", 512, _F), ("c1", 256, _F), ("c2", 256, _F), ("o1", 128, _F), ("o2", 128, _F),
        ("ox", 2048, _F), ("dd", 2048, _B), ("da", 2048, _B), ("db", 2048, _B), ("mt", 2048, _B),
        ("eb", 128, _F), ("key", 128, _F), ("kt", 128, _F), ("ks", 128, _F), ("et", 128, _H), ("rt", 128, _H),
        ("l1", 8, _U), ("l2", 32, _U), ("dl2", 8, _F), ("w2", 8, _F), ("w2b", 8, _F),
        ("win", 128, _B), ("wj", 128, _B), ("cab", 4, _B),
        ("ah", 128, _I), ("al", 128, _I), ("ak", 128, _I), ("ap", 128, _F), ("as2", 128, _F), ("ad", 128, _F), ("ea", 128, _F),
        ("ac1", 128, _F), ("ac2", 128, _F),
        ("bg", 128, _F), ("bh", 128, _I), ("bl", 128, _I), ("bk", 128, _I), ("bs", 128, _F), ("bp", 128, _F), ("di", 128, _F),
        ("dq", 128, _F), ("sg", 128, _F), ("ebz", 128, _F), ("bd2", 128, _F), ("t2b", 128, _F), ("pp", 128, _F), ("d2", 128, _F)]:
    SCRATCH[_n] = ("sbuf", [128, _w], _d)
for _n, _w, _d in [("idf", 128, _F), ("trb", 512, _B), ("big", 1024, _B), ("pb", 1024, _B), ("pc", 1024, _H), ("nc", 1024, _H), ("wg", 240, _B),
                   ("sq", 512, _B), ("eq", 1024, _B), ("aa", 4, _F)]:
    SCRATCH[_n] = ("sbuf", [128, _w], _d)
for _n in ("ji", "sb", "key"):
    SCRATCH.pop(_n)
for _n in ("psU", "psK0", "psK1", "psL", "psR", "psC", "psG", "psV"):
    SCRATCH[_n] = ("psum", [128, 512], _F)
SEMAPHORES = (["sV", "sA", "sP", "sG", "dent", "dsm", "dfe", "dy", "loc"]
              + ["%s%d" % (k, t) for k in ("ro", "re", "rn", "ra") for t in range(RO)])


def rank_program(g, core, T, topo):
    rank = T.rank_of(core)
    if rank is None:
        return
    A = AluOpType
    F = ActivationFunctionType
    Q = {"V": g.vector, "A": g.scalar, "P": g.tensor, "G": g, "S": g.sync}
    tot = {}
    seen = {"V": {}, "A": {}, "P": {}, "G": {}, "S": {}}
    wr, rd, bank = {}, {}, {}
    v, a, pe = g.vector, g.scalar, g.tensor

    def wait(q, evs):
        evs = [e for e in evs if seen[q].get(e[0], 0) < e[1]]
        for e in evs:
            if seen[q].get(e[0], 0) >= e[1]:
                continue
            if any(o is not e and o[2].get(e[0], 0) >= e[1] and (o[0] != e[0] or o[1] > e[1]) for o in evs):
                continue
            Q[q].wait_ge(T.sem[e[0]], e[1])
            seen[q][e[0]] = e[1]
        for e in evs:
            for s, n in e[2].items():
                if seen[q].get(s, 0) < n:
                    seen[q][s] = n

    def deps(q, r, w):
        evs = []
        for k in r:
            evs += [e for o, e in wr.get(k, [])]
        for k in w:
            evs += [e for o, e in wr.get(k, []) if o != q]
            evs += [e for o, e in rd.get(k, []) if o != q]
        for k in list(r) + list(w):
            if k[:2] == "ps":
                evs += [e for o, e in bank.get(k.split(":")[0], {}).items() if o != q]
        return evs

    def note(q, r, w, ev):
        for k in w:
            wr[k] = [(q, ev)]
            rd[k] = []
        for k in r:
            rd[k] = [x for x in rd.get(k, []) if x[0] != q or q == "D"] + [(q, ev)]
        for k in list(r) + list(w):
            if k[:2] == "ps":
                bank.setdefault(k.split(":")[0], {})[q] = ev

    def op(q, fn, r, w):
        wait(q, deps(q, r, w))
        s = "s" + q
        tot[s] = tot.get(s, 0) + 1
        fn().then_inc(T.sem[s], 1)
        clk = dict(seen[q])
        clk[s] = tot[s]
        note(q, r, w, (s, tot[s], clk))

    def dma(q, out, in_, r, w, s):
        wait(q, deps("D" + q, r, w))
        Q[q].dma_start(out, in_).then_inc(T.sem[s], 16)
        tot[s] = tot.get(s, 0) + 16
        clk = dict(seen[q])
        clk[s] = tot[s]
        note("D", r, w, (s, tot[s], clk))

    def joined(k, s):
        wr[k] = [("D", (s, tot[s], {s: tot[s]}))]

    def send(dst, out, in_, r, s):
        wait("G", deps("G", r, []))
        rid, pid = topo.addr(dst)[:2]
        m = 0
        for e in topo.engines(core, dst)[:NE]:
            m |= 1 << e
        g.remote_dma(out, in_, T.sem[s], T.sem["loc"], pid, rid, m)
        tot["loc"] = tot.get("loc", 0) + NE

    def landed(k, s):
        tot[s] = NE
        wr[k] = [("R", (s, NE, {s: NE}))]

    def ts(out, in0, s1, s2, o0, o1, r, w):
        if o1 is None:
            op("V", lambda: v.tensor_scalar(out, in0, s1, None, o0), r, w)
        else:
            op("V", lambda: v.tensor_scalar(out, in0, s1, s2, o0, o1), r, w)

    def tt(out, i0, i1, o, r, w):
        op("V", lambda: v.tensor_tensor(out, i0, i1, o), r, w)

    def vc(out, in_, r, w):
        op("V", lambda: v.tensor_copy(out, in_), r, w)

    def act(out, in_, f, r, w, bias=0.0, scale=1.0):
        op("A", lambda: a.activation(out, in_, f, bias=bias, scale=scale), r, w)

    def mm(out, l, rh, st, sp, r, w):
        op("P", lambda: pe.matmul(out, l, rh, st, sp), r, w)

    def ms(ap, c, w):
        op("V", lambda: v.memset(ap, c), [], w)

    BC = {}

    def bias(c):
        if c not in BC:
            i = len(BC)
            BC[c] = i
            ms(T.bcol[:, i:i + 1], c, ["bc%d" % i])
        return T.bcol[:, BC[c]:BC[c] + 1]

    dma("S", T.ents[:, 0:1024], T.ent[:, 0:1024], [], [], "dent")
    dma("A", T.ents[:, 1024:2048], T.ent[:, 1024:2048], [], [], "dent")
    joined("ents", "dent")
    dma("S", T.wti[:, 0:1], T.wt[:, 0:1], [], [], "dsm")
    dma("A", T.kpi[:, 0:1], T.kap[:, 0:1], [], [], "dsm")
    joined("wti", "dsm")
    joined("kpi", "dsm")
    dma("S", T.fw[:, 0:2048], T.feat[:, 0:2048], [], [], "dfe")
    dma("A", T.fw[:, 2048:4096], T.feat[:, 2048:4096], [], [], "dfe")
    joined("fw", "dfe")

    ms(T.ones[:], 1.0, ["ones"])
    ms(T.big[:], 4096.0, ["big"])
    op("G", lambda: g.iota(T.sti[:], [[37, 64]], 0, 0), [], ["sti"])
    op("G", lambda: g.iota(T.pi[:, 0:1], [[1, 1]], 0, 1), [], ["pi"])
    op("G", lambda: g.affine_select(T.bd0[:], T.ones[:, 0:128], [[-16, 8], [0, 16]], A.is_ge, 0.0, 0, 1), ["ones"], ["bd0"])
    op("G", lambda: g.affine_select(T.bd[:], T.bd0[:], [[16, 8], [0, 16]], A.is_ge, 0.0, 15, -1), ["bd0"], ["bd"])
    op("G", lambda: g.iota(T.cli[:], [[1, 128]], 0, 0), [], ["cli"])
    op("G", lambda: g.affine_select(T.z0[:], T.ones[:, 0:144], [[-16, 9], [0, 16]], A.is_ge, 0.0, 0, 1), ["ones"], ["z0"])
    op("G", lambda: g.affine_select(T.z1[:], T.z0[:], [[16, 9], [0, 16]], A.is_ge, 0.0, 15, -1), ["z0"], ["z1"])
    op("G", lambda: g.affine_select(T.z2[:], T.z1[:], [[0, 9], [1, 16]], A.is_equal, 0.0, -15, 0), ["z1"], ["z2"])
    op("G", lambda: g.affine_select(T.iz[:], T.ones[:], [[-1, 160]], A.is_equal, 0.0, 16, 1), ["ones"], ["iz"])
    op("G", lambda: g.iota(T.ii[:], [[16, 8]], 2048, 0), [], ["ii"])
    op("G", lambda: g.affine_select(T.trb[:], T.big[:, 0:512], [[0, 4], [-1, 128]], A.is_ge, 0.0, 0, 1), ["big"], ["trb"])
    op("G", lambda: g.affine_select(T.pb[:], T.big[:], [[-16, 8], [0, 128]], A.is_equal, 0.0, -15, 1), ["big"], ["pb"])
    ts(T.stj[:], T.sti[:], 63, None, A.bitwise_and, None, ["sti"], ["stj"])
    ts(T.st[:, 0:64], T.stj[:], 2048.0, -17.0, A.mult, A.add, ["stj"], ["st"])
    n = 64
    while n < 2048:
        act(T.st[:, n:2 * n], T.st[:, 0:n], F.Copy, ["st"], ["st"])
        n *= 2
    b_w, b_f, b_w1, b_mb, b_mmb, b_64, b_ea, b_one, b_15, b_m32 = [
        bias(c) for c in (-8.5, M16, -1024.5, MB, -MB, -64.0, 1.0 / BIG, 1.0, -15.5, M0 * 32)]
    wait("A", [wr["bc%d" % i][0][1] for i in range(len(BC))])
    ms(T.fm[:], 1.0, ["fm"])
    op("V", lambda: v.memset(T.fm[:, 0:2048:16], 0.0), ["fm"], ["fm"])
    ms(T.fw[:, 4096:4112], 0.0, ["fwz"])
    ms(T.pcol[:, 8:9], 0.0, ["acol"])
    ts(T.p16[:, 0:1], T.pi[:, 0:1], 15, None, A.bitwise_and, None, ["pi"], ["p16"])
    ts(T.p16[:, 1:2], T.pi[:, 0:1], 16, None, A.bitwise_and, None, ["pi"], ["p16b"])
    ts(T.pcol[:, 3:4], T.p16[:, 0:1], -2048.0, 15 * 2048 - 1023.5, A.mult, A.add, ["p16"], ["pc3"])
    vc(T.cl[:], T.cli[:], ["cli"], ["cl"])
    vc(T.pcol[:, 6:7], T.wti[:, 0:1], ["wti"], ["wcol"])
    vc(T.pcol[:, 7:8], T.kpi[:, 0:1], ["kpi"], ["kcol"])
    ts(T.wblk[:], T.bd[:], T.pcol[:, 6:7], None, A.mult, None, ["bd", "wcol"], ["wblk"])

    def more_constants():
        ms(T.one16[:], 0.0625, ["one16"])
        ms(T.sa[:], 0.0, ["sa"])
        vc(T.pcol[:, 0:1], T.p16[:, 0:1], ["p16"], ["pc0"])
        ts(T.pcol[:, 1:2], T.p16[:, 1:2], 0.0, None, A.is_equal, None, ["p16b"], ["pc1"])
        ts(T.pcol[:, 2:3], T.p16[:, 1:2], 0.0, None, A.is_gt, None, ["p16b"], ["pc2"])
        ts(T.pc[:], T.pb[:], 2.0 ** -12, None, A.mult, None, ["pb"], ["pc"])
        ts(T.nc[:], T.pb[:], -2.0 ** -12, None, A.mult, None, ["pb"], ["nc"])
        ms(T.wg[:], 0.0, ["wg0"])
        op("V", lambda: v.memset(T.wg[:, 112:128], 1.0), ["wg0"], ["wg"])
        ts(T.zl[:], T.z2[:], 0.0625, None, A.mult, None, ["z2"], ["zl"])
        ts(T.iz0[:], T.iz[:], T.pcol[:, 1:2], None, A.mult, None, ["iz", "pc1"], ["iz0"])
        ts(T.iz1[:], T.iz[:], T.pcol[:, 2:3], None, A.mult, None, ["iz", "pc2"], ["iz1"])
        ts(T.dum[:], T.ii[:], T.pcol[:, 0:1], None, A.add, None, ["ii", "pc0"], ["dum"])
        yield
        ts(T.dmc[:], T.dum[:], -1023.5, None, A.add, None, ["dum"], ["dmc"])
        for i in range(4):
            s = slice(512 * i, 512 * i + 512)
            vc(T.raw[:, s], T.ents[:, s], ["ents"], ["raw"])
            if i % 2:
                yield

    banks = ["psK0", "psK1", "psR", "psC"]

    def first_parts(blocks):
        for i in blocks:
            s = slice(512 * i, 512 * i + 512)
            k = "@%d" % i
            ts(T.cf1[:, s], T.ents[:, s], -1024.5, MB, A.add, A.add, ["ents"], ["cf1" + k])
            act(T[banks[i]][:], T.cf1[:, s], F.Identity, ["cf1" + k], [banks[i]], bias=b_mmb)
            ts(T.cf2[:, s], T.ents[:, s], -8.5, M16, A.add, A.add, ["ents"], ["cf2" + k])

    def first_cod():
        for i in range(4):
            s = slice(512 * i, 512 * i + 512)
            tt(T.cod[:, s], T[banks[i]][:], T.cf2[:, s], A.add, [banks[i], "cf2@%d" % i], ["cod"])

    def code_parts(src, sk, t1, t2, k, ps):
        act(t2, src, F.Identity, sk, [k + "2"], bias=b_w)
        act(t1, src, F.Identity, sk, [k + "1"], bias=b_w1)
        act(t2, t2, F.Identity, [k + "2"], [k + "2"], bias=b_f)
        act(t1, t1, F.Identity, [k + "1"], [k + "1"], bias=b_mb)
        act(ps, t1, F.Identity, [k + "1"], [("psG:" if k == "n" else "psL:") + k], bias=b_mmb)

    def lane_list(t):
        src, sk = (T.ents, "ents") if t == 0 else (T.raw, "raw")
        ts(T.i1[:], src[:, t:2048:16], -1.0, None, A.add, None, [sk], ["i1"])
        ts(T.i3[:], T.i1[:], 16, None, A.bitwise_and, None, ["i1"], ["i3"])
        ts(T.i2[:], T.i1[:], 11, None, A.arith_shift_right, None, ["i1"], ["i2"])
        ts(T.psV[:, 0:128], T.i3[:], 512.0, None, A.mult, None, ["i3"], ["psV:1"])
        tt(T.psV[:, 128:256], T.i2[:], T.psV[:, 0:128], A.add, ["i2", "psV:1"], ["psV:2"])
        ts(T.lst[:], T.psV[:, 128:256], 4096.0, None, A.min, None, ["psV:2"], ["lst"])

    def own_parts(t):
        o = 256 * t
        if t == 0:
            vc(T.so[:, 0:128], T.ents[:, 0:2048:16], ["ents"], ["so0"])
        else:
            act(T.so[:, o:o + 128], T.raw[:, t:2048:16], F.Copy, ["raw"], ["so%d" % t])
        code_parts(T.so[:, o:o + 128], ["so%d" % t], T.o1[:], T.o2[:], "o", T.psL[:, 256:384])

    def own_send(t, dst):
        o = 256 * t
        tt(T.so[:, o + 128:o + 256], T.psL[:, 256:384], T.o2[:], A.add, ["psL:o", "o2"], ["soc%d" % t])
        send(dst, T.lo[:, o:o + 256], T.so[:, o:o + 256], ["so%d" % t, "soc%d" % t], "ro%d" % t)

    def features(vs):
        rk = ["lst", "fw", "fwz"]
        op("A", lambda: a.activation(T.fg[:, 16 * vs:2048], T.fw[:].indirect(T.lst[:, vs:128]), F.Copy), rk, ["fgA"])
        op("V", lambda: v.tensor_copy(T.fg[:, 0:16 * vs], T.fw[:].indirect(T.lst[:, 0:vs])), rk, ["fgV"])

    def scans(vs):
        for n0, n1, k in ((0, vs, "V"), (vs, 128, "A")):
            c = slice(16 * n0, 16 * n1)
            op("V", lambda: v.tensor_tensor_scan(T.fs[:, c], T.fm[:, c], T.fg[:, c], 0.0, A.mult, A.max), ["fm", "fg" + k], ["fs" + k])
        mm(T.psU[:, 0:128], T.wblk[:], T.fs[:, 15:2048:16], True, True, ["wblk", "fsV", "fsA"], ["psU"])

    def cand(t, dst):
        o = 128 * t
        ac, ak = (T.pcol[:, 8:9], "acol") if t == 0 else (T.la[:, 4 * t - 4:4 * t - 3], "la%d" % (t - 1))
        vc(T.u1[:], T.psU[:, 0:128], ["psU"], ["u1"])
        ts(T.u2[:], T.u1[:], 4095, None, A.bitwise_and, None, ["u1"], ["u2"])
        ts(T.psV[:, 0:128], T.u2[:], 0.03125, T.pcol[:, 7:8], A.mult, A.add, ["u2", "kcol"], ["psV:1"])
        tt(T.u4[:], T.psV[:, 0:128], T.u2[:], A.mult, ["psV:1", "u2"], ["u4"])
        ts(T.u5[:], T.u4[:], ac, -0.375, A.add, A.add, ["u4", ak], ["u5"])
        ts(T.u6[:], T.u5[:], 2047, None, A.bitwise_and, None, ["u5"], ["u6"])
        vc(T.se[:, o:o + 128], T.u6[:], ["u6"], ["se%d" % t])
        send(dst, T.le[:, o:o + 128], T.se[:, o:o + 128], ["se%d" % t], "re%d" % t)

    def scatter(tab, lists, vals, r):
        op("V", lambda: v.tensor_copy(T[tab][:].indirect(lists), vals), r, [tab])

    def own_side(t):
        o = 256 * t
        th = 8.0 + t
        av, lk = T.lo[:, o:o + 128], "lo%d" % t
        tt(T.ah[:], av, T.st[:, t:2048:16], A.add, [lk, "st"], ["ah"])
        ts(T.al[:], T.ah[:], 31, None, A.bitwise_and, None, ["ah"], ["al"])
        ts(T.ak[:], T.ah[:], 114688, None, A.bitwise_and, None, ["ah"], ["ak"])
        ts(T.psV[:, 0:128], T.al[:], th, BIG, A.is_ge, A.mult, ["al"], ["psV:1"])
        ts(T.psV[:, 256:384], T.al[:], 16.0, None, A.is_ge, None, ["al"], ["psV:ia"])
        tt(T.psV[:, 128:256], T.ak[:], T.psV[:, 0:128], A.is_le, ["ak", "psV:1"], ["psV:2"])
        tt(T.as2[:], T.al[:], T.psV[:, 0:128], A.add, ["al", "psV:1"], ["as2"])
        tt(T.psV[:, 384:512], av, T.psV[:, 0:128], A.mult, [lk, "psV:1"], ["psV:ga"])
        tt(T.ap[:], av, T.psV[:, 128:256], A.mult, [lk, "psV:2"], ["ap"])

    def own_side_scalar(t):
        act(T.ad[:], T.as2[:], F.Relu, ["as2"], ["ad"], bias=b_ck[t], scale=-1.0)
        act(T.ac1[:], T.ap[:], F.Identity, ["ap"], ["ac1"], bias=b_w1)
        act(T.ea[:], T.ap[:], F.Relu, ["ap"], ["ea"], bias=b_ea, scale=-1.0 / BIG)
        act(T.ac2[:], T.ac1[:], F.Identity, ["ac1"], ["ac2"], bias=b_mb)
        act(T.psG[:, 384:512], T.ac2[:], F.Identity, ["ac2"], ["psG:c"], bias=b_mmb)

    def expand(t, h):
        o = 256 * t + 128
        op("A", lambda: a.activation(T.ox[:, 1024 * h:1024 * h + 1024],
                                     T.lo[:, o:o + 128].indirect(T.cl[:, 64 * h:64 * h + 64]), F.Copy),
           ["lo%d" % t, "cl"], ["ox%d" % h])

    CH = [0, 32, 64, 104, 128]
    todo = [more_constants()]

    def fill():
        return next(todo[0], 1) is None

    def score(t):
        def gat(i):
            c = slice(16 * CH[i], 16 * CH[i + 1])
            o = 128 * t
            op("V", lambda: v.tensor_tensor(T.dd[:, c], T.cod[:, 0:2048].indirect(T.le[:, o + CH[i]:o + CH[i + 1]]), T.ox[:, c], A.subtract),
               ["cod", "le%d" % t, "ox%d" % (i // 2)], ["dd%d" % i])
            act(T.da[:, c], T.dd[:, c], F.Abs, ["dd%d" % i], ["da%d" % i], scale=0.0625)
            if i > 1:
                act(T.db[:, c], T.da[:, c], F.Abs, ["da%d" % i], ["db%d" % i], bias=b_64)

        def thr(i):
            c = slice(16 * CH[i], 16 * CH[i + 1])
            if i > 1:
                ts(T.mt[:, c], T.db[:, c], 63.75, None, A.is_lt, None, ["db%d" % i], ["mt%d" % i])
            else:
                ts(T.mt[:, c], T.da[:, c], 127.5, None, A.is_lt, None, ["da%d" % i], ["mt%d" % i])

        def same(i):
            c = slice(16 * CH[i], 16 * CH[i + 1])
            ts(T.db[:, c], T.da[:, c], 0.5, None, A.is_lt, None, ["da%d" % i], ["db%d" % i])

        def add(h):
            k = "psK0:k%d" % h
            s = slice(64 * h, 64 * h + 64)
            mm(T.psK0[:, s], T.idf[:], T.eb[:, s], True, False, ["idf", "eb"], [k])
            for m in range(16):
                mm(T.psK0[:, s], T.z[:, 15 - m:143 - m], T.mt[:, 1024 * h + m:1024 * h + 1024:16], False, m == 15 and h == 1,
                   ["z", "mt%d" % (2 * h), "mt%d" % (2 * h + 1)], [k])

        def sub():
            for m in range(16):
                mm(T.psK0[:, 0:64], T.zn[:, 15 - m:143 - m], T.db[:, m:1024:16], False, m == 15,
                   ["zn", "db0", "db1"], ["psK0:k0"])

        gat(0)
        gat(1)
        ts(T.eb[:], T.le[:, 128 * t:128 * t + 128], T.pcol[:, 3:4], None, A.add, None, ["le%d" % t, "pc3"], ["eb"])
        gat(2)
        thr(0)
        thr(1)
        add(0)
        gat(3)
        same(0)
        same(1)
        sub()
        fill()
        thr(2)
        fill()
        thr(3)
        add(1)
        while fill():
            pass

    def partner(t):
        for i, k in enumerate(("psU", "psR")):
            mm(T[k][:], T.iz[:, 16:144], T.trb[:], True, False, ["iz", "trb"], [k + ":d"])
        op("V", lambda: v.transpose(T.kt[:], T.psK0[:, 0:128]), ["psK0:k0", "psK0:k1"], ["kt"])
        op("V", lambda: v.tensor_tensor_scan(T.ks[:], T.fm[:, 0:128], T.kt[:], 0.0, A.mult, A.max), ["fm", "kt"], ["ks"])
        ts(T.psK1[:, 0:128], T.ks[:], MB, -MB, A.add, A.add, ["ks"], ["psK1:0"])
        tt(T.et[:], T.ks[:], T.psK1[:, 0:128], A.subtract, ["ks", "psK1:0"], ["et"])
        for h in range(2):
            for g2 in range(2):
                b = 16 - 16 * (g2 - h)
                mm(T.psL[:, h:8:2], T["iz%d" % h][:, b:b + 128], T.et[:, 16 * g2 + 15:128:32], g2 == 0, g2 == 1,
                   ["iz%d" % h, "et"], ["psL"])
        op("V", lambda: v.transpose(T.rt[:], T.et[:]), ["et"], ["rt"])
        for i, k in enumerate(("psU", "psR")):
            mm(T[k][:], T.rt[:], T.nc[:, 512 * i:512 * i + 512], False, False, ["rt", "nc"], [k + ":d"])
            for b in range(4):
                c = 512 * i + 128 * b
                mm(T[k][:, 128 * b:128 * b + 128], T.pc[:, c:c + 128], T.rt[:], False, b == 3, ["rt", "pc"], [k + ":d"])
        act(T.sq[:], T.psU[:], F.Square, ["psU:d"], ["sq"])
        act(T.eq[:, 0:512], T.sq[:], F.Relu, ["sq"], ["eq0"], bias=b_one, scale=-1.0)
        ts(T.l1[:], T.psL[:, 0:8], 1023.5, None, A.add, None, ["psL"], ["l1"])
        tt(T.dl2[:], T.psL[:, 0:8], T.dmc[:], A.subtract, ["psL", "dmc"], ["dl2"])
        op("V", lambda: v.tensor_copy(T.bg[:], T.raw[:, 0:2048].indirect(T.l1[:])), ["raw", "l1"], ["bg"])
        op("V", lambda: v.tensor_tensor(T.bh[:], T.st[:].indirect(T.l1[:]), T.bg[:], A.add), ["st", "l1", "bg"], ["bh"])

    K0, K1 = T.psK0, T.psK1

    def meet(t, dst):
        th = 8.0 + t
        X = 384 * t
        last = t == RO - 1
        ts(T.bl[:], T.bh[:], 31, None, A.bitwise_and, None, ["bh"], ["bl"])
        ts(T.bk[:], T.bh[:], 114688, None, A.bitwise_and, None, ["bh"], ["bk"])
        ts(K0[:, 0:128], T.bl[:], th, BIG, A.is_ge, A.mult, ["bl"], ["psK0:bn"])
        ts(K1[:, 0:128], T.bl[:], 16.0, None, A.is_ge, None, ["bl"], ["psK1:0"])
        tt(K0[:, 128:256], T.bk[:], K0[:, 0:128], A.is_le, ["bk", "psK0:bn"], ["psK0:bv"])
        tt(T.bs[:], T.bl[:], K0[:, 0:128], A.add, ["bl", "psK0:bn"], ["bs"])
        act(T.bd2[:], T.bs[:], F.Relu, ["bs"], ["bd2"], bias=b_ck[t], scale=-1.0)
        tt(T.bp[:], T.bg[:], K0[:, 128:256], A.mult, ["bg", "psK0:bv"], ["bp"])
        ts(T.eq[:, 512:1024], T.psR[:], 0.0, None, A.is_equal, None, ["psR:d"], ["eq1"])
        for c in range(8):
            mm(T.psC[:, 0:128], T.wg[:, 112 - 16 * c:240 - 16 * c], T.eq[:, 128 * c:128 * c + 128], c == 0, c == 7,
               ["wg", "eq%d" % (c // 4)], ["psC"])
        tt(T.di[:], T.bp[:], T.psG[:, 384:512], A.subtract, ["bp", "psG:c"], ["di"])
        act(T.dq[:], T.di[:], F.Square, ["di"], ["dq"], bias=b_sq, scale=1.0 / 1024)
        act(T.sg[:], T.dq[:], F.Sign, ["dq"], ["sg"], bias=b_one, scale=-1.0)
        act(T.ebz[:], T.bp[:], F.Relu, ["bp"], ["ebz"], bias=b_ea, scale=-1.0 / BIG)
        act(T.win[:], T.psC[:, 0:128], F.Relu, ["psC"], ["win"], bias=b_one, scale=-1.0)
        for s in range(16):
            mm(T.psC[:, 128:136], T.zl[:, 15 - s:143 - s], T.win[:, s:128:16], s == 0, s == 15, ["zl", "win"], ["psC:l"])
        if not last:
            op("A", lambda: a.activation(T.wj[:], T.win[:], F.Copy, accum_out=T.pcol[:, 9:10]), ["win"], ["wj", "ca"])
            act(T.cab[:, 0:1], T.pcol[:, 9:10], F.Copy, ["ca"], ["cab"])
            mm(T.psC[:, 136:137], T.one16[:], T.cab[:, 0:1], True, True, ["one16", "cab"], ["psC:a"])
            pa = T.psC[:, 136:137]
            act(T.aa[:, 0:1], pa, F.Identity, ["psC:a"], ["aa0"], bias=b_15)
            act(T.aa[:, 1:2], T.aa[:, 0:1], F.Identity, ["aa0"], ["aa1"], bias=b_m32)
            act(T.aa[:, 2:3], T.aa[:, 1:2], F.Identity, ["aa1"], ["aa2"], bias=b_m32, scale=-1.0)
            act(T.sa[:, 4 * t:4 * t + 1], pa, F.Identity, ["psC:a", "aa2", "sa"], ["sa%d" % t], bias=T.aa[:, 2:3])
            send(dst, T.la[:, 4 * t:4 * t + 4], T.sa[:, 4 * t:4 * t + 4], ["sa", "sa%d" % t], "ra%d" % t)
        tt(K0[:, 256:384], T.bg[:], K0[:, 0:128], A.mult, ["bg", "psK0:bn"], ["psK0:gb"])
        tt(K1[:, 128:256], K1[:, 0:128], T.ad[:], A.mult, ["psK1:0", "ad"], ["psK1:1"])
        tt(K1[:, 256:384], T.bd2[:], T.psV[:, 256:384], A.mult, ["bd2", "psV:ia"], ["psK1:2"])
        tt(K1[:, 0:128], K1[:, 128:256], T.ap[:], A.add, ["psK1:1", "ap"], ["psK1:3"])
        tt(T.t2b[:], K1[:, 256:384], T.bp[:], A.add, ["psK1:2", "bp"], ["t2b"])

        def a_new1():
            tt(K0[:, 384:512], K0[:, 256:384], T.ea[:], A.mult, ["psK0:gb", "ea"], ["psK0:x"])
            tt(K0[:, 0:128], K0[:, 384:512], T.ap[:], A.max, ["psK0:x", "ap"], ["psK0:y"])
            tt(K0[:, 128:256], K0[:, 0:128], T.pp[:], A.max, ["psK0:y", "pp"], ["psK0:z"])
            tt(T.d2[:], K0[:, 128:256], T.lo[:, 256 * t:256 * t + 128], A.subtract, ["psK0:z", "lo%d" % t], ["d2"])

        def a_new2():
            tt(K0[:, 256:384], T.d2[:], T.win[:], A.mult, ["d2", "win"], ["psK0:w"])
            tt(T.sx[:, X + 128:X + 256], K0[:, 256:384], T.lo[:, 256 * t:256 * t + 128], A.add, ["psK0:w", "lo%d" % t], ["na%d" % t])

        tt(K1[:, 128:256], T.t2b[:], K1[:, 0:128], A.max, ["t2b", "psK1:3"], ["psK1:4"])
        tt(K1[:, 256:384], T.ebz[:], T.psV[:, 384:512], A.mult, ["ebz", "psV:ga"], ["psK1:5"])
        tt(T.pp[:], K1[:, 128:256], T.sg[:], A.mult, ["psK1:4", "sg"], ["pp"])
        a_new1()
        if last:
            a_new2()
            send(dst, T.ln[:, 256 * t:256 * t + 128], T.sx[:, X + 128:X + 256], ["na%d" % t], "rn%d" % t)
        tt(K1[:, 384:512], K1[:, 256:384], T.bp[:], A.max, ["psK1:5", "bp"], ["psK1:6"])
        tt(T.w2[:], T.psC[:, 128:136], T.dl2[:], A.mult, ["psC:l", "dl2"], ["w2"])
        tt(T.sx[:, X:X + 128], K1[:, 384:512], T.pp[:], A.max, ["psK1:6", "pp"], ["nb%d" % t])
        tt(T.w2b[:], T.w2[:], T.dum[:], A.add, ["w2", "dum"], ["w2b"])
        vc(T.l2[:, 8 * t:8 * t + 8], T.w2b[:], ["w2b"], ["l2%d" % t])
        if last:
            return
        scatter("raw", T.l2[:, 8 * t:8 * t + 8], T.sx[:, X:X + 128], ["l2%d" % t, "nb%d" % t])
        meet_rest.append(a_new2)

    meet_rest = []

    def new_parts(t):
        X = 384 * t
        code_parts(T.sx[:, X:X + 256], ["nb%d" % t, "na%d" % t], T.c1[:], T.c2[:], "n", T.psG[:, 0:256])

    def finish(t, dst):
        X = 384 * t
        tt(T.sx[:, X + 256:X + 384], T.psG[:, 128:256], T.c2[:, 128:256], A.add, ["psG:n", "n2"], ["nc%d" % t])
        tt(T.nbc[:, 128 * t:128 * t + 128], T.psG[:, 0:128], T.c2[:, 0:128], A.add, ["psG:n", "n2"], ["nbc%d" % t])
        send(dst, T.ln[:, 256 * t:256 * t + 256], T.sx[:, X + 128:X + 384], ["na%d" % t, "nc%d" % t], "rn%d" % t)

    def back_scalar(t):
        o = 256 * t
        lk = "ln%d" % t
        act(T.raw[:, t:2048:16], T.ln[:, o:o + 128], F.Copy, [lk], ["raw"])
        if t < RO - 1:
            act(T.cod[:, t:2048:16], T.ln[:, o + 128:o + 256], F.Copy, [lk], ["cod"])

    def back(t):
        X = 384 * t
        l2 = T.l2[:, 8 * t:8 * t + 8]
        if t < RO - 1:
            scatter("cod", l2, T.nbc[:, 128 * t:128 * t + 128], ["l2%d" % t, "nbc%d" % t, "cod"])
        scatter("raw", l2, T.sx[:, X:X + 128], ["l2%d" % t, "nb%d" % t, "raw"])

    b_sq = T.pcol[:, 11:12]
    b_ck = [T.pcol[:, 12 + t:13 + t] for t in range(RO)]
    for t in range(RO):
        callee = T.cores[(rank + 1 + t % 7) % N]
        caller = T.cores[(rank - 1 - t % 7) % N]
        landed("lo%d" % t, "ro%d" % t)
        landed("le%d" % t, "re%d" % t)
        landed("ln%d" % t, "rn%d" % t)
        if t < RO - 1:
            landed("la%d" % t, "ra%d" % t)
        own_parts(t)
        lane_list(t)
        vs = VS if t else VS0
        features(vs)
        own_send(t, callee)
        if t == 0:
            first_parts((0, 1))
        else:
            meet_rest.pop()()
            new_parts(t - 1)
        scans(vs)
        if t:
            finish(t - 1, prev)
        cand(t, callee)
        if t == 0:
            first_parts((2, 3))
            ts(T.z[:], T.z2[:], 32768.0, None, A.mult, None, ["z2"], ["z"])
            vc(T.idf[:], T.iz[:, 16:144], ["iz"], ["idf"])
            ts(T.zn[:], T.z2[:], -32768.0, None, A.mult, None, ["z2"], ["zn"])
            ms(b_sq, -1024.5 / 1024, ["bx1"])
            for i in range(RO):
                ms(b_ck[i], 12.0 + i, ["bx2"])
            first_cod()
        expand(t, 0)
        expand(t, 1)
        own_side(t)
        if t:
            back_scalar(t - 1)
            back(t - 1)
        score(t)
        if t == 0:
            wait("A", [wr[k][0][1] for k in ("bx1", "bx2")])
        own_side_scalar(t)
        partner(t)
        meet(t, caller)
        prev = caller
    back_scalar(RO - 1)
    back(RO - 1)
    dma("S", T.yent[:, 0:1024], T.raw[:, 0:1024], ["raw"], [], "dy")
    dma("A", T.yent[:, 1024:2048], T.raw[:, 1024:2048], ["raw"], [], "dy")
    for s in tot:
        wait("G", [(s, tot[s], {})])
